import numpy as np, ml_dtypes
CORES = [2,6,10,14,18,22,26,30]
N = 8
import mx_ref
BF = ml_dtypes.bfloat16
def gentries(a):
    return np.ascontiguousarray(a.reshape(8, 16, -1).transpose(0, 2, 1)).reshape(8, -1)
def gtable(e):
    e = np.asarray(e); return np.ascontiguousarray(e.reshape(8, -1, 16).transpose(0, 2, 1)).reshape(128, -1).astype(np.int32)
def gcols(t, e):
    v = np.concatenate([t.reshape(8, 16, -1, 4), np.zeros((8, 16, 1, 4), BF)], axis=2)
    return np.ascontiguousarray(np.stack([v[g][:, e[g]] for g in range(8)])).reshape(128, -1)
def tile(rs):
    return np.stack(rs, axis=2).reshape(128, -1).astype(BF)
def cut(t, i, w=512):
    return t[:, w * i:w * i + w]
def pick(q, e):
    c = np.concatenate([q[0].reshape(128, -1, 4), np.zeros((128, 1, 4), np.uint8)], axis=1); s = np.concatenate([q[1], np.ones((16, 1), np.uint8)], axis=1)
    return (np.ascontiguousarray(c[:, e].reshape(128, -1)), np.ascontiguousarray(s[:, e]))
def join(*qs):
    return (np.concatenate([q[0] for q in qs], axis=1), np.concatenate([q[1] for q in qs], axis=1))
def put(q, e, v):
    c, s = q[0].reshape(128, -1, 4).copy(), q[1].copy(); c[:, e] = v[0].reshape(128, -1, 4); s[:, e] = v[1]
    return (c.reshape(128, -1), s)
def pk(c, s):
    return (np.ascontiguousarray(c), mx_ref.live(s))
def emit(q):
    return q[0], q[1]
def packed(v, rng):
    q = [mx_ref.quantize(np.ascontiguousarray(v[r])) for r in range(N)]
    return np.stack([a for a, b in q]), np.stack([mx_ref.plane(b, rng) for a, b in q])
def values_of_codes():
    e, c = np.zeros((128, 128, 4), np.float32), np.zeros((128, 2, 4), np.uint8)
    e[np.arange(128), np.arange(128), 0] = 1
    c[:127, :, 0] = np.arange(256).reshape(2, 128).T[:127]
    return mx_ref.matmul(mx_ref.quantize(e.reshape(128, 512).astype(BF)), (c.reshape(128, 8), np.full((16, 2), 127, np.uint8))).T.reshape(-1).astype(np.float64)
CODE_VALUE, SCALE_VALUE = values_of_codes(), 2.0 ** (np.arange(256) - 127.0)
def decode(q):
    return (CODE_VALUE[q[0]].reshape(16, 8, -1, 4) * SCALE_VALUE[q[1]][:, None, :, None] + 0.0).reshape(128, -1).astype(np.float32)
def f(rng, *shape):
    return mx_ref.flush((rng.standard_normal(shape, dtype=np.float32) * np.exp2(rng.integers(-2, 3, shape[:-1] + (1,)))).astype(BF))
def wide(rng, *shape, cols=0):
    v = rng.standard_normal(shape, dtype=np.float32) * np.exp2(rng.integers(-12, 13, shape)).astype(np.float32)
    if cols: v *= np.repeat(np.exp2(rng.integers(-cols, cols + 1, shape[:-2] + (1, shape[-1] // 4))) * (rng.random(shape[:-2] + (1, shape[-1] // 4)) > 0.0625), 4, axis=-1).astype(np.float32)
    return mx_ref.flush(v.astype(BF))
C, V, B, R = 512, 8, 64, 3
def big(v):
    v = v.astype(np.float32)
    v[np.abs(v) < np.float32(2.0 ** -16)] = 0
    return v.astype(BF)
def numbers_of(rng):
    return {"x": big(f(rng, N, 128, 4 * C)), "u": np.array(f(rng, N, 128, 512)), "v": np.array(f(rng, N, 128, 512))}
def weights(rng, still=[]):
    w = big(f(rng, N, 128, 2048)).reshape(N, 8, 16, 4, 8, 16, 4)
    for i in still:
        w[:, :, i] = 0
        w[:, :, :, :, :, i] = 0
    c, p = packed(w.reshape(N, 128, 2048), rng)
    return {"wc": c, "ws": p}
def yards(h, p):
    return {"hg": np.stack([gtable(h[r].reshape(8, 3 * B)) for r in range(N)]), "dg": np.stack([gtable(p[r]) for r in range(N)])}
def heights(rng):
    c = np.sort(rng.integers(0, V + 1, (N, 8, 2, B)), axis=2)
    return np.concatenate([c[:, :, :1], c[:, :, 1:] - c[:, :, :1], V - c[:, :, 1:]], axis=2)
def deals(rng):
    return np.argsort(rng.random((N, 8, C)), axis=2)
def signs(rng):
    return np.stack([rng.permutation(8) % 2 * 2.0 - 1.0 for r in range(N)])
def setup_inputs(rng):
    return {**numbers_of(rng), **weights(rng), **yards(heights(rng), deals(rng))}
def setup_inputs_ties(rng):
    d = numbers_of(rng)
    e = rng.permutation(N)
    x = d["x"].reshape(N, 8, 16, C, 4)
    for r in range(N):
        k = np.zeros(C, int) if r == e[0] else rng.permutation(C) % 3
        a = x[r][:, :8, :3].copy()
        a[:, :, 2] = 0
        x[r][:, :8] = a[:, :, k]
    x[e[1]] = 0
    u = d["u"].reshape(N, 8, 16, 8, 16, 4)
    k = u.copy()
    u[:, :, :, :, 0] = 0
    for g in range(8): u[:, g, :8, g, 0] = k[:, g, :8, g, 0]
    return {"x": x.reshape(N, 128, 4 * C), "u": u.reshape(N, 128, 512), "v": d["v"], **weights(rng, range(8)), **yards(heights(rng), deals(rng))}
def setup_inputs_near(rng):
    d = numbers_of(rng)
    x = d["x"].astype(np.float32).reshape(N, 8, 16, C, 4)
    u = d["u"].reshape(N, 128, 128, 4)
    x[:, :, 0] = 0
    u[:, :, ::16] = 0
    o, c = rng.permutation(N) % 4, signs(rng)
    for r in range(N):
        t = (V - 1 - (np.arange(V) + rng.integers(0, V, (8, B, 1))) % V).reshape(8, C)
        s = t // 2
        size = 1.0 if o[r] < 2 else 2.0 ** -4
        if o[r] < 2:
            x[r, :, 0, :, 0] = c[r][:, None]
            for i in rng.permutation(8)[:4]: x[r, i, 0, rng.integers(C), 0] *= np.float32(2.0 ** 30)
        if o[r] == 3:
            x[r, :, 1:8] = 0
            x[r, :, 0, :, 0] = (8 + t % 2) * 2.0 ** -30
        x[r, :, 8] = ((s[:, :, None] >> np.arange(4)) & 1) * np.exp2(np.arange(4) - 23.0) * size
        x[r, :, 9:] = rng.integers(4, 8, (8, 7, C, 4)) * 2.0 ** -20 * size
        k = 1.0 if o[r] == 0 else 2.0 ** -30
        for h in range(0, 128, 16):
            u[r, h, h, 0] = k
            u[r, h + 8, h] = k
    return {"x": x.reshape(N, 128, 4 * C).astype(BF), "u": u.reshape(N, 128, 512), "v": d["v"], **weights(rng, [0, 8, 9, 10, 11, 12, 13, 14, 15]), **yards(heights(rng), deals(rng))}
def setup_inputs_stacks(rng):
    d = numbers_of(rng)
    x = d["x"].reshape(N, 8, 16, C, 4)
    u = d["u"].reshape(N, 128, 128, 4)
    h, s = np.zeros((N, 8, 3, B), int), rng.integers(4, 8, (N, 8, B, V))
    for r in range(N):
        for g in range(8):
            c = rng.permutation(B) % 6
            for i in range(B):
                a, l, o = rng.permutation(3)
                m = int(rng.integers(1, V - 2))
                w = np.zeros(3, int)
                w[[a, l, o]] = [(V, 0, 0), (V, 0, 0), (1, V - 1, 0), (V - 2, 0, 2), (V - 2, 1, 1), (2, m, V - 2 - m)][c[i]]
                h[r, g, :, i] = w
                b = [0, w[0], w[0] + w[1]]
                k = s[r, g, i]
                k[b[a] + (V - 1 if c[i] == 1 else 0)] = 1
                if c[i] == 4: k[b[l]] = k[b[o]]
                if c[i] == 5: k[b[o] + rng.integers(w[o])] = 2
    s[rng.permutation(N) < N // 2] -= 12
    x[:, :, 0] = 0
    x[:, :, 0, :, 0] = s.reshape(N, 8, C).astype(np.float32).astype(BF)
    u[:, :, ::16] = 0
    for j in range(0, 128, 16): u[:, j, j, 0] = 1
    p, e = deals(rng), rng.permutation(N)
    p[e[0]] = np.arange(C)
    p[e[1]] = np.arange(C)[::-1]
    return {"x": x.reshape(N, 128, 4 * C), "u": u.reshape(N, 128, 512), "v": d["v"], **weights(rng, [0]), **yards(h, p)}
def setup_inputs_huge(rng):
    d = numbers_of(rng)
    x = 2.0 ** 30 * (0.8 + 0.2 * rng.random((N, 128, C, 4)))
    c = np.stack([rng.permutation(C) % 2 * 2.0 - 1.0 for r in range(N)])
    c[rng.permutation(N) < N // 2] = 1
    x *= c[:, None, :, None]
    u = d["u"].reshape(N, 128, 128, 4)
    a = 2.0 ** 30 * (1 - 0.1 * rng.random((N, 128, 8, 4))) * signs(rng)[:, None, :, None]
    u[:, :, ::16] = a.astype(np.float32).astype(BF)
    w = np.zeros((N, 128, 4, 128, 4), np.float32)
    i = np.arange(128)
    for b in range(4): w[:, i, b, i, b] = -1
    wc, ws = packed(w.reshape(N, 128, 2048).astype(BF), rng)
    return {"x": x.astype(np.float32).reshape(N, 128, 4 * C).astype(BF), "u": u.reshape(N, 128, 512), "v": d["v"], "wc": wc, "ws": ws, **yards(heights(rng), deals(rng))}
def setup_inputs_spread(rng):
    d = setup_inputs(rng)
    d["x"] = big(wide(rng, N, 128, 4 * C, cols=6))
    return d
def check_inputs(d):
    b = []
    for k in ("x", "u", "v"):
        a = np.abs(d[k].astype(np.float32))
        if not (np.isfinite(a).all() and ((a == 0) | (a >= 2.0 ** -30) & (a <= 2.0 ** 30)).all()): b.append("a value of " + k)
    if ((d["wc"] & 0x7F) == 0x7F).any(): b.append("a code of wc that is no number")
    none, least, most = [emit(mx_ref.quantize(np.full((128, 16), k, np.float32).astype(BF)))[1][0, 0] for k in (0.0, 2.0 ** -30, 2.0 ** 30)]
    for r in range(N):
        s = mx_ref.live(d["ws"][r])
        if ((s != none) & ((s < least) | (s > most))).any(): b.append("a scale of ws")
        h = gentries(d["hg"][r]).reshape(8, 3, B)
        if (h < 0).any() or (h > V).any() or (np.sum(h, axis=1) != V).any(): b.append("the heights hg")
        if (np.sort(gentries(d["dg"][r]), axis=1) != np.arange(C)).any(): b.append("dg: no permutation")
    return b
def reference(x, u, v, wc, ws, hg, dg):
    qu = [mx_ref.quantize(u[r]) for r in range(N)]
    lay = [pk(wc[r], ws[r]) for r in range(N)]
    now = [x[r] for r in range(N)]
    high = [gentries(hg[r]).reshape(8, 3, B).transpose(0, 2, 1) for r in range(N)]
    place, three, start = np.arange(V), np.arange(3), V * np.arange(B)[:, None]
    for t in range(R):
        sent, moved = [], []
        for r in range(N):
            s = (mx_ref.matmul(qu[r], mx_ref.quantize(now[r]))[::16] + np.float32(0.0)).reshape(8, B, V)
            h = high[r]
            end = np.stack([h[:, :, 0], h[:, :, 0] + h[:, :, 1], np.full((8, B), V)], axis=2)
            stack = (place >= end[:, :, :1]).astype(int) + (place >= end[:, :, 1:2])
            k = np.argmin(s, axis=2)[:, :, None]
            a = np.take_along_axis(stack, k, axis=2)
            low = np.stack([np.min(np.where(stack == i, s, np.float32(np.inf)), axis=2) for i in range(3)], axis=2)
            low[three == a] = -np.inf
            l = np.argmax(low, axis=2)[:, :, None]
            up = (stack == a) & (place > k)
            m = np.where(up & (np.take_along_axis(h, l, axis=2) > 0), np.take_along_axis(end, l, axis=2) - 1, place)
            key = np.where(up, 4 * V * l + 2 * V - place, 4 * V * stack + place)
            key = np.where(place == k, 4 * V * a + 3 * V, key)
            o = np.argsort(key, axis=2)
            high[r] = h + np.sum(up, axis=2)[:, :, None] * ((three == l).astype(int) - (three == a).astype(int))
            moved.append(((start + o).reshape(8, C), (start + np.take_along_axis(m, o, axis=2)).reshape(8, C), (o == k).reshape(8, C)))
            sent.append(mx_ref.quantize(gcols(now[r], (start + k).reshape(8, B))))
        came = decode(join(*sent)).astype(BF)
        for r in range(N):
            c = np.ascontiguousarray(cut(came, (r - 1) % N, 4 * B))
            q = mx_ref.quantize(c)
            new = tile([mx_ref.matmul(pick(lay[r], np.arange(128 * b, 128 * b + 128)), q) * np.float32(0.015625) + c[:, b::4].astype(np.float32) for b in range(4)])
            e, m, arrived = moved[r]
            z = ((gcols(now[r], e).astype(np.float32) + gcols(now[r], m).astype(np.float32)) * np.float32(0.5)).astype(BF)
            yard = np.where(arrived, C + np.arange(C) // V, np.arange(C))
            now[r] = gcols(np.concatenate([z, new], axis=1), np.take_along_axis(yard, gentries(dg[r]), axis=1))
    y, oh = np.zeros((N, 128, C), np.float32), np.zeros((N, 8, 3 * B), np.float32)
    oc, osc = np.zeros((N, 128, 4 * C), np.uint8), np.zeros((N, 16, C), np.uint8)
    for r in range(N):
        q = mx_ref.quantize(now[r])
        y[r] = mx_ref.matmul(mx_ref.quantize(v[r]), q)
        oh[r] = high[r].transpose(0, 2, 1).reshape(8, 3 * B)
        oc[r], osc[r] = emit(q)
    return {"y": y, "oh": oh, "oc": oc, "osc": osc}

@@ -1,0 +1,416 @@
+from concourse.mybir import dt, AluOpType, ActivationFunctionType
+
+F32, BF, I32, U16, U8, CODE = "float32", "bfloat16", "int32", "uint16", "uint8", "float8_e4m3fn_x4"
+R = 3
+PL = 1088
+BIG = 2.0 ** 99
+FAR = 2.0 ** 20
+SUMS = [(0, 0, 18), (7, 10, 16), (7, 10, 16)]
+PLAN = [("v", 0, 0, 256), ("a", 2, 0, 256), ("v", 1, 0, 256), ("a", 3, 0, 256), ("v", 0, 256, 512), ("a", 2, 256, 512), ("q", 0, 0, 256),
+        ("a", 3, 256, 512), ("a", 1, 256, 384), ("v", 1, 384, 512), ("q", 0, 256, 512)]
+LAST = [("v", 0, 0, 256), ("a", 2, 0, 256), ("v", 1, 0, 256), ("a", 3, 0, 256), ("q", 0, 0, 256),
+        ("a", 0, 256, 384), ("a", 1, 256, 384), ("v", 2, 256, 384), ("v", 3, 256, 384), ("y", "a", 0, 256), ("q", 1, 256, 384),
+        ("a", 0, 384, 512), ("v", 2, 384, 512), ("a", 1, 384, 512), ("v", 3, 384, 512), ("y", "a", 256, 384), ("q", 2, 384, 512), ("y", "v", 384, 512)]
+A_SPLIT = 8
+
+
+def _sb(n, t):
+    return ("sbuf", [128, n], t)
+
+
+SCRATCH = {
+    "ub": _sb(512, BF), "vb": _sb(512, BF), "uq": _sb(128, CODE), "us": _sb(128, U8), "vq": _sb(128, CODE), "vs": _sb(128, U8),
+    "wq": _sb(512, CODE), "wp": _sb(512, U8), "ec": _sb(528, BF), "eb": _sb(528, BF), "eq": _sb(512, CODE), "es": _sb(512, U8),
+    "xq": _sb(512, CODE), "xs": _sb(512, U8), "at": _sb(512, BF), "gt": _sb(512, BF), "gq": _sb(128, CODE), "gs": _sb(128, U8),
+    "mg": _sb(256, BF), "yb": _sb(512, F32), "c6": _sb(64, F32), "y4": _sb(64, F32), "mb": _sb(64, F32), "moff": _sb(16, U16),
+    "src": _sb(48, I32), "si": _sb(96, I32), "sf": _sb(64, F32), "ta": _sb(48, F32), "tb": _sb(48, F32), "o0": _sb(32, F32), "o1": _sb(32, F32),
+    "pi": _sb(1, I32), "bi": _sb(8, I32), "bf": _sb(16, F32), "cc": _sb(24, F32), "kk": _sb(96, F32), "rst": _sb(96, F32), "rm": _sb(32, F32),
+    "c4": _sb(32, F32), "yp": _sb(32, F32), "ab": _sb(32, F32), "off": _sb(32, U16), "loff": _sb(32, U16), "aoff": _sb(16, U16), "em16": _sb(32, U16),
+    "st": _sb(128, F32), "p4": _sb(128, BF), "zs": _sb(64, BF), "tt": _sb(512, F32), "sc": _sb(64, F32), "pm": _sb(64, F32), "ge": _sb(32, F32), "wb": _sb(48, F32),
+    "a1": _sb(32, F32), "a2": _sb(32, F32), "a3": _sb(16, F32), "m1": _sb(64, F32), "m2": _sb(64, F32), "m3": _sb(48, F32),
+    "pen": _sb(96, F32), "gz": _sb(64, F32), "gd": _sb(32, F32), "ms": _sb(96, F32), "low": _sb(96, F32),
+    "mx": _sb(8, F32), "l0": _sb(4, F32), "fl": _sb(24, F32), "zz": _sb(16, F32), "pr": _sb(16, F32), "dd": _sb(48, F32), "up": _sb(32, F32),
+    "pb": _sb(128, BF), "tab": _sb(128, BF), "pg": _sb(512, BF), "pt": _sb(512, BF), "e2": _sb(320, BF), "en": _sb(160, F32),
+    "df": _sb(16, F32), "ht": _sb(32, F32), "ho": _sb(32, F32),
+}
+for _r in range(R + 1):
+    SCRATCH["xt%d" % _r] = _sb(2048, BF)
+for _r in range(R):
+    SCRATCH["xh%d" % _r] = _sb(4 * PL, BF)
+    SCRATCH["cq%d" % _r] = _sb(192, CODE)
+    SCRATCH["cs%d" % _r] = _sb(192, U8)
+for _b in range(8):
+    SCRATCH["ps%d" % _b] = ("psum", [128, 512], F32)
+
+SEMAPHORES = ["sv", "sa", "sp", "sg", "lx0", "lx1", "ll", "lu", "lw", "lv", "sto", "sent", "arr0", "arr1", "arr2"]
+
+
+def rank_program(g, core, T, topo):
+    rank = T.rank_of(core)
+    if rank is None:
+        return
+    A = AluOpType
+    ACT = ActivationFunctionType
+    n_ranks = len(T.cores)
+    nxt = T.cores[(rank + 1) % n_ranks]
+    eng = {"v": g.vector, "a": g.scalar, "p": g.tensor, "g": g, "s": g.sync}
+    own = {"v": "sv", "a": "sa", "p": "sp", "g": "sg"}
+    count = {"sv": 0, "sa": 0, "sp": 0, "sg": 0}
+    known = {q: {} for q in eng}
+    hist = {}
+
+    def v(name, a=0, b=None, s=1):
+        if b is None:
+            b = SCRATCH[name][1][1]
+        return (T[name][:, a:b:s] if s > 1 else T[name][:, a:b], [(name, frozenset(range(a, b, s)))])
+
+    def ind(win, off):
+        return (win[0].indirect(off[0]), win[1] + off[1])
+
+    def wait(q, tok):
+        if known[q].get(tok[0], 0) < tok[1]:
+            eng[q].wait_ge(T.sem[tok[0]], tok[1])
+            known[q][tok[0]] = tok[1]
+        for s, n in tok[2].items():
+            if known[q].get(s, 0) < n:
+                known[q][s] = n
+
+    def order(q, reads, writes, free=False):
+        toks = []
+        for spans, w in ((reads, False), (writes, True)):
+            for name, el in spans:
+                for el2, w2, q2, tok in hist.get(name, []):
+                    if name.startswith("ps"):
+                        if q2 != q or ((w or w2) and not free):
+                            toks.append(tok)
+                    elif (w or w2) and not el.isdisjoint(el2):
+                        toks.append(tok)
+        for tok in sorted(toks, key=lambda t: -t[1]):
+            wait(q, tok)
+
+    def note(q, reads, writes, tok):
+        for spans, w in ((reads, False), (writes, True)):
+            for name, el in spans:
+                hist.setdefault(name, []).append((el, w, q, tok))
+
+    def op(q, fn, out, ins, free=False):
+        reads = [s for i in ins for s in i[1]]
+        writes = [s for o in out for s in o[1]]
+        order(q, reads, writes, free)
+        s = own[q]
+        fn().then_inc(T.sem[s], 1)
+        count[s] += 1
+        note(q, reads, writes, (s, count[s], dict(known[q])))
+
+    def load(q, out, in_, sem, total, codes=False):
+        eng[q].dma_start(out[0].bitcast(dt.uint8) if codes else out[0], in_).then_inc(T.sem[sem], 16)
+        note(sem, [], out[1], (sem, total, {}))
+
+    stores = [0]
+
+    def store(q, out, in_, view):
+        order(q, view[1], [])
+        eng[q].dma_start(out, in_).then_inc(T.sem.sto, 16)
+        stores[0] += 16
+
+    def tt(o, a, b, alu):
+        op("v", lambda: g.vector.tensor_tensor(o[0], a[0], b[0], alu), [o], [a, b])
+
+    def ts(o, a, s1, op0, s2=None, op1=None):
+        ins = [a] + [s for s in (s1, s2) if isinstance(s, tuple)]
+        x1 = s1[0] if isinstance(s1, tuple) else s1
+        x2 = s2[0] if isinstance(s2, tuple) else s2
+        if op1 is None:
+            op("v", lambda: g.vector.tensor_scalar(o[0], a[0], x1, None, op0), [o], ins)
+        else:
+            op("v", lambda: g.vector.tensor_scalar(o[0], a[0], x1, x2, op0, op1), [o], ins)
+
+    def cp(o, a):
+        op("v", lambda: g.vector.tensor_copy(o[0], a[0]), [o], [a])
+
+    def tr(o, a):
+        op("v", lambda: g.vector.transpose(o[0], a[0]), [o], [a])
+
+    def scan(o, d0, d1, op0, op1):
+        op("v", lambda: g.vector.tensor_tensor_scan(o[0], d0[0], d1[0], 0.0, op0, op1), [o], [d0, d1])
+
+    def fill(o, c):
+        op("v", lambda: g.vector.memset(o[0], c), [o], [])
+
+    def quant(c, s, t):
+        op("v", lambda: g.vector.quantize_mx(c[0], s[0], t[0]), [c, s], [t])
+
+    def act(o, a, scale=None, bias=None):
+        if bias is not None:
+            op("a", lambda: g.scalar.activation(o[0], a[0], ACT.Identity, bias=bias, scale=scale), [o], [a])
+        elif scale is None:
+            op("a", lambda: g.scalar.activation(o[0], a[0], ACT.Copy), [o], [a])
+        else:
+            op("a", lambda: g.scalar.activation(o[0], a[0], ACT.Copy, scale=scale), [o], [a])
+
+    def mm(o, lq, ls, rq, rs, start=True, stop=True):
+        op("p", lambda: g.tensor.matmul_mx(o[0], lq[0], ls[0], rq[0], rs[0], start, stop), [o], [lq, ls, rq, rs], free=not start)
+
+    def iota(o, pattern, base, cm, flt=True):
+        if flt:
+            op("g", lambda: g.iota(o[0], pattern, base, cm, allow_small_or_imprecise_dtypes=True), [o], [])
+        else:
+            op("g", lambda: g.iota(o[0], pattern, base, cm), [o], [])
+
+    def bytes_of(view):
+        return view[0].bitcast(dt.uint8)
+
+    load("a", v("src", 32, 44), T.hg[:, :], "ll", 32)
+    load("s", v("xt0", 0, 1024), T.x[:, 0:1024], "lx0", 16)
+    load("a", v("src", 0, 32), T.dg[:, :], "ll", 32)
+    load("s", v("xt0", 1024, 2048), T.x[:, 1024:2048], "lx1", 16)
+    load("a", v("ub"), T.u[:, :], "lu", 16)
+    load("s", v("wq"), T.wc[:, :], "lw", 32, codes=True)
+    load("s", v("wp"), T.ws[:, :], "lw", 32)
+    load("s", v("vb"), T.v[:, :], "lv", 16)
+
+    fill(v("ec"), 64.0)
+    iota(v("pi"), [[0, 1]], 0, 1, flt=False)
+    iota(v("cc", 0, 6), [[0, 3], [16, 2]], 0, 0)
+    iota(v("cc", 6, 14), [[0, 2], [4, 2], [16, 2]], 0, 0)
+    iota(v("kk"), [[0, 12], [-1, 8]], 8, 0)
+    iota(v("c4"), [[0, 4], [1024, 2], [1, 4]], 32, 0)
+    iota(v("yp"), [[0, 2], [1, 2], [0, 8]], 0, 0)
+    iota(v("cc", 16, 20), [[1, 2], [2, 2]], 36, 0)
+    iota(v("c6"), [[1024, 2], [0, 8], [1, 4]], 28, 0)
+    iota(v("y4"), [[0, 4], [1, 4], [0, 4]], 0, 0)
+    op("g", lambda: g.affine_select(v("eb")[0], v("ec")[0], [[-1, 528]], A.is_equal, 0.0, 3, 4), [v("eb")], [v("ec")])
+    act(v("sf", 44, 64), v("ec", 0, 20), 0.0)
+    act(v("at", 256, 512), v("ec", 0, 256), 0.0)
+    act(v("gt", 256, 512), v("ec", 0, 256), 0.0)
+    act(v("pb"), v("ec", 0, 128), 0.0)
+    act(v("ht"), v("ec", 0, 32), 0.0)
+    act(v("zs"), v("ec", 0, 64), 0.0)
+    for r in range(R):
+        act(v("xh%d" % r, 1, 4 * PL, 16), v("ec", 0, 4 * PL // 16), 0.0)
+    for i, m in enumerate((7, 8, 4, 6, 31, 1, 3)):
+        ts(v("bi", i, i + 1), v("pi"), m, A.bitwise_and)
+    cp(v("bf", 0, 7), v("bi", 0, 7))
+    b7, b8, b4, b6, b31, b1, b3, x0, x1, x2, x3, x4 = (v("bf", i, i + 1) for i in range(12))
+    CL, BL, AL, ML, CD, DL, GL, NL = (v("off", a, b) for a, b in ((0, 4), (4, 6), (6, 8), (8, 14), (14, 15), (16, 19), (20, 24), (24, 28)))
+    ts(v("rst"), v("kk"), 8.0, A.is_equal, BIG, A.mult)
+    ts(x0, b7, 16.0, A.mult, b8, A.add)
+    ts(x1, b4, 2.0, A.mult, 7.0, A.add)
+    ts(x2, b31, 8.0, A.mult)
+    ts(x3, b8, 0.5, A.mult, 32.0, A.add)
+    ts(x4, b8, 0.125, A.mult, 6.0, A.add)
+    ts(v("rm"), v("kk", 0, 32), 8.0, A.not_equal)
+    ts(CL, v("cc", 6, 14, 2), x0, A.add, 4.0, A.mult)
+    ts(BL, v("cc", 0, 2), b8, A.add, 7.0, A.add)
+    ts(AL, v("cc", 0, 2), x1, A.add)
+    ts(v("a1"), v("c4"), 0.25, A.mult, x2, A.add)
+    ts(v("a2"), v("yp"), b1, A.not_equal, -FAR, A.mult)
+    ts(GL, v("cc", 6, 10), b8, A.add, 0.25, A.mult)
+    tt(v("ab"), v("a1"), v("a2"), A.add)
+    ts(ML, v("cc", 0, 6), b7, A.add, b8, A.add)
+    ts(CD, b6, 4.0, A.mult, 7.0, A.add)
+    ts(v("off", 16, 17), b6, 0.5, A.mult, x3, A.add)
+    ts(v("off", 17, 18), b6, 4.0, A.mult, x4, A.add)
+    ts(v("off", 18, 19), b6, 0.5, A.mult, 40.0, A.add)
+    cp(NL, v("cc", 16, 20))
+    ts(v("m1"), v("c6"), 0.25, A.mult, x2, A.add)
+    ts(v("m2"), v("y4"), b3, A.not_equal, -FAR, A.mult)
+    tt(v("mb"), v("m1"), v("m2"), A.add)
+
+    PF, PM, HC, SX = (v("st", 32 * i, 32 * i + 32) for i in range(4))
+    D = v("src", 0, 32)
+    ts(v("si", 0, 32), D, 3, A.logical_shift_right)
+    cp(v("sf", 32, 44), v("src", 32, 44))
+    ts(v("si", 32, 64), D, 7, A.bitwise_and)
+    cp(v("sf", 0, 32), v("si", 0, 32))
+    cp(PF, v("si", 32, 64))
+    tr(v("tb", 0, 32), v("sf", 0, 64, 2))
+    tr(v("ta", 16, 48), v("sf", 1, 64, 2))
+    for i in range(4):
+        act(v("p4", i, 128, 4), PF, -1.0, 7.0 if i == 2 else 8.0)
+    act(PM, PF, -1.0, 7.0)
+    act(v("zs", 0, 64, 2), PF, -2.0, 15.0)
+    cp(v("ta", 0, 16), v("tb", 0, 16))
+    cp(v("tb", 32, 48), v("ta", 32, 48))
+    tr(v("o0"), v("ta", 0, 32))
+    tr(v("o1"), v("tb", 16, 48))
+    quant(v("uq"), v("us"), v("ub"))
+    for par in range(2):
+        o = "o%d" % par
+        ts(v("zz", 4 * par, 4 * par + 4, 2), v(o, 16, 18), -1.0, A.mult, 8.0, A.add)
+        cp(v("zz", 4 * par + 1, 4 * par + 4, 2), v(o, 20, 22))
+    quant(v("xq", 0, 256), v("xs", 0, 256), v("xt0", 0, 1024))
+    cp(v("zz", 8, 16), v("zz", 0, 8))
+    quant(v("xq", 256, 512), v("xs", 256, 512), v("xt0", 1024, 2048))
+
+    def entry_tables():
+        ts(v("si", 64, 96), D, 3, A.logical_shift_right, 31, A.bitwise_and)
+        ts(SX, D, 256.0, A.is_ge, 0.5, A.mult)
+        ts(HC, v("si", 64, 96), 512.0, A.add)
+        quant(v("vq"), v("vs"), v("vb"))
+        tt(HC, HC, SX, A.add)
+
+    def penalties():
+        tt(v("gz"), ind(v("zz", 0, 8), GL), v("kk", 0, 64), A.is_ge)
+        ts(v("pen", 0, 32), v("gz", 0, 32), BIG, A.mult)
+        tt(v("gd"), v("gz", 32, 64), v("gz", 0, 32), A.is_ge)
+        ts(v("pen", 64, 96), v("gz", 32, 64), -BIG, A.mult, BIG, A.add)
+        ts(v("pen", 32, 64), v("gd"), BIG, A.mult)
+
+    def doubles(r, t):
+        act(v("xh%d" % r, PL * t, PL * t + 1024, 2), v("xt%d" % r, t, 2048, 4), 2.0)
+
+    n_eng = min(len(topo.engines(T.cores[i], T.cores[(i + 1) % n_ranks])) for i in range(n_ranks))
+    mask = sum(1 << e for e in topo.engines(core, nxt)[:n_eng])
+    rid, pid, _se = topo.addr(nxt)
+
+    for r in range(R):
+        xt, xh, cq, cs, xn = "xt%d" % r, "xh%d" % r, "cq%d" % r, "cs%d" % r, "xt%d" % (r + 1)
+        mm(v("ps0"), v("uq"), v("us"), v("xq"), v("xs"))
+        penalties()
+        for t in range(3 if r == 0 else 4):
+            doubles(r, t)
+        for k in range(8):
+            tr(v("tt", 64 * k, 64 * k + 64), v("ps0", k, 512, 8))
+        cp(v("sc"), ind(v("tt"), CL))
+        scan(v("pm"), v("rst", 0, 64), v("sc"), A.add, A.min)
+        tt(v("ms"), ind(v("sc", 0, 32), ML), v("pen"), A.add)
+        tt(v("ge"), ind(v("pm", 0, 32), BL), v("pm", 32, 64), A.is_ge)
+        scan(v("low"), v("rst"), v("ms"), A.add, A.min)
+        scan(v("wb", 0, 32), v("rm"), v("ge"), A.mult, A.add)
+        tt(v("mx"), v("low", 7, 64, 8), v("low", 39, 96, 8), A.max)
+        tt(v("a1"), ind(v("wb", 0, 32), AL), v("ab"), A.subtract)
+        tt(v("fl", 0, 16), ind(v("wb", 0, 32), CD), v("zz"), A.is_gt)
+        tr(v("a2"), v("a1"))
+        tt(v("l0"), v("low", 7, 32, 8), v("mx", 4, 8), A.is_ge)
+        tt(v("a3"), v("a2", 0, 32, 2), v("a2", 1, 32, 2), A.min)
+        tt(v("fl", 17, 24, 2), v("mx", 0, 4), v("low", 71, 96, 8), A.is_ge)
+        ts(v("aoff"), v("a3"), -4.0, A.mult)
+        if A_SPLIT < 16:
+            act(v("at", 16 * A_SPLIT, 256), ind(v(xt), v("aoff", A_SPLIT, 16)))
+        tt(v("fl", 16, 24, 2), v("l0"), v("fl", 8, 16, 2), A.is_gt)
+        if A_SPLIT:
+            cp(v("at", 0, 16 * A_SPLIT), ind(v(xt), v("aoff", 0, A_SPLIT)))
+        tt(v("pr"), v("fl", 8, 24), v("zz"), A.mult)
+        if A_SPLIT < 8:
+            tt(v("wb", 40, 44), v("mx", 0, 4), v("mx", 4, 8), A.max)
+            tt(v("wb", 32, 40), v("pr", 0, 16, 2), v("pr", 1, 16, 2), A.max)
+            tt(v("df", 0, 8), v("fl", 8, 16), v("fl", 16, 24), A.subtract)
+        quant(v(cq, 64, 192), v(cs, 64, 192), v("at"))
+        order("g", v(cq, 64, 128)[1] + v(cs, 64, 128)[1], [])
+        g.remote_dma(bytes_of(v(cq, 0, 64)), bytes_of(v(cq, 64, 128)), T.sem["arr%d" % r], T.sem.sent, pid, rid, mask)
+        g.remote_dma(v(cs, 0, 64)[0], v(cs, 64, 128)[0], T.sem["arr%d" % r], T.sem.sent, pid, rid, mask)
+        note("far", [], v(cq, 0, 64)[1] + v(cs, 0, 64)[1], ("arr%d" % r, 2 * n_eng, {}))
+        if A_SPLIT >= 8:
+            tt(v("wb", 32, 40), v("pr", 0, 16, 2), v("pr", 1, 16, 2), A.max)
+            tt(v("wb", 40, 44), v("mx", 0, 4), v("mx", 4, 8), A.max)
+        tt(v("m1"), ind(v("wb", 0, 44), NL), v("mb"), A.subtract)
+        cp(v("dd"), ind(v("wb", 0, 44), DL))
+        ZA, ZL, C1, C, MM = (v("dd", 8 * i, 8 * i + 8) for i in range(5))
+        B0, B1, HP, T2, BS, NN = (v("pb", i, 128, 16) for i in (0, 4, 8, 12, 1, 9))
+        UP, NU, FL, BZ = (v("up", 8 * i, 8 * i + 8) for i in range(4))
+        tr(v("m2"), v("m1"))
+        tt(NN, C1, ZA, A.subtract)
+        tt(v("m3", 0, 32), v("m2", 0, 64, 2), v("m2", 1, 64, 2), A.min)
+        tt(UP, ZL, C, A.is_lt)
+        tt(v("m3", 32, 48), v("m3", 0, 32, 2), v("m3", 1, 32, 2), A.min)
+        tt(NU, NN, UP, A.mult)
+        ts(v("moff"), v("m3", 32, 48), -4.0, A.mult, 0.0, A.max)
+        act(v("mg"), ind(v(xt), v("moff")))
+        ts(FL, MM, BIG / 2, A.is_lt, 0.5, A.mult)
+        tt(B0, ZL, NU, A.add)
+        tt(BZ, FL, ZA, A.subtract)
+        tt(B1, B0, NN, A.subtract)
+        tt(HP, ZA, NU, A.add)
+        tt(T2, B1, NU, A.add)
+        tt(BS, BZ, B0, A.subtract)
+        if A_SPLIT >= 8:
+            tt(v("df", 0, 8), v("fl", 8, 16), v("fl", 16, 24), A.subtract)
+        tr(v("tab"), v("pb"))
+        if r == 0:
+            for par in range(2):
+                ts(v("loff", par, 32, 2), v("o%d" % par, 0, 16), 64.0 * par, A.add)
+        act(v("pg", 0, 256), ind(v("tab"), v("loff", 0, 16)))
+        act(v("pg", 256, 512), ind(v("tab"), v("loff", 16, 32)))
+        if r == 0:
+            doubles(0, 3)
+            for b in range(4):
+                quant(v("eq", 128 * b, 128 * b + 128), v("es", 128 * b, 128 * b + 128), v("eb", 3 - b, 515 - b))
+            entry_tables()
+        for b in range(8):
+            e = b % 4
+            mm(v("ps%d" % b, 0, 128), v("eq", 128 * e, 128 * e + 128), v("es", 128 * e, 128 * e + 128), v(cq, 0, 128), v(cs, 0, 128), True, b < 4)
+        for b in range(4):
+            act(v("gt", b, 256, 4), v("ps%d" % b, 0, 64), 2.0 ** -6)
+        done = [0]
+
+        def sums(upto):
+            while done[0] < upto:
+                t, k = divmod(done[0], 7)
+                tt(v(xh, PL * t + 2 * k + 3, PL * t + 1024, 16), v(xt, 4 * k + 4 + t, 2048, 32), v("mg", t, 256, 4), A.add)
+                done[0] += 1
+        tt(v("df", 8, 16), v("df", 0, 8), NN, A.mult)
+        sums(SUMS[r][0])
+        tr(v("pt", 0, 256), v("pg", 0, 256))
+        tt(v("zz", 0, 8), v("zz", 0, 8), v("df", 8, 16), A.add)
+        if r < R - 1:
+            tt(v("zz", 8, 16), v("zz", 8, 16), v("df", 8, 16), A.add)
+        sums(SUMS[r][1])
+        tr(v("pt", 256, 512), v("pg", 256, 512))
+        sums(done[0] + 1)
+        tt(v("e2", 0, 128), v("pt", 0, 512, 4), v("p4"), A.is_ge)
+        tt(v("e2", 192, 256), v("pt", 1, 512, 8), v("zs"), A.add)
+        tt(v("e2", 128, 192), v("e2", 0, 128, 2), v("e2", 1, 128, 2), A.subtract)
+        tt(v("en", 0, 32), v("pt", 8, 512, 16), PM, A.is_equal)
+        tt(v("e2", 256, 320), v("e2", 128, 192), v("e2", 192, 256), A.mult)
+        tt(v("en", 32, 64), v("en", 0, 32), HC, A.mult)
+        tt(v("en", 64, 96), v("e2", 256, 320, 2), v("e2", 257, 320, 2), A.add)
+        sums(done[0] + 1)
+        tt(v("en", 96, 128), v("en", 64, 96), D, A.add)
+        sums(done[0] + 1)
+        tt(v("en", 128, 160), v("en", 96, 128), v("en", 32, 64), A.max)
+        sums(done[0] + 1)
+        ts(v("em16"), v("en", 128, 160), 2.0, A.mult)
+        sums(SUMS[r][2])
+        quant(v("gq"), v("gs"), v("gt"))
+        for b in range(4):
+            mm(v("ps%d" % (4 + b), 0, 128), v("wq", 128 * b, 128 * b + 128), v("wp", 128 * b, 128 * b + 128), v("gq"), v("gs"), False, True)
+        for b in range(4):
+            act(v(xh, PL * b + 1024, PL * b + PL), v("ps%d" % (4 + b), 0, 64), 2.0 ** -5)
+        if r == R - 1:
+            for h in range(2):
+                z0, z1 = v("zz", 2 * h, 8, 4), v("zz", 2 * h + 1, 8, 4)
+                ts(v("ht", h, 12, 6), z0, -1.0, A.mult, 8.0, A.add)
+                tt(v("ht", 2 + h, 12, 6), z0, z1, A.subtract)
+                cp(v("ht", 4 + h, 12, 6), z1)
+            sums(done[0] + 1)
+            tr(v("ho"), v("ht"))
+            for a in range(4):
+                store("s", T.oh[2 * a:2 * a + 2, :], T.ho[32 * a:32 * a + 12, :], v("ho"))
+        sums(28)
+        bank = {}
+        for kind, t, a, b in (PLAN if r < R - 1 else LAST):
+            if kind == "q":
+                quant(v("xq", a, b), v("xs", a, b), v(xn, 4 * a, 4 * b))
+                if r == R - 1:
+                    bank[a] = "ps%d" % t
+                    mm(v(bank[a], 0, b - a), v("vq"), v("vs"), v("xq", a, b), v("xs", a, b))
+                    store("s", T.oc[:, 4 * a:4 * b], bytes_of(v("xq", a, b)), v("xq", a, b))
+                    if b == 512:
+                        for k in range(4):
+                            store("s", T.osc[4 * k:4 * k + 4, :], T.xs[32 * k:32 * k + 4, :], v("xs"))
+            elif kind == "y":
+                (cp if t == "v" else act)(v("yb", a, b), v(bank[a], 0, b - a))
+                store("a", T.y[:, a:b], v("yb", a, b)[0], v("yb", a, b))
+            else:
+                src = ind(v(xh, PL * t, PL * t + PL), v("em16", a // 16, b // 16))
+                dst = v(xn, 4 * a + t, 4 * b, 4)
+                if kind == "v":
+                    ts(dst, src, 0.5, A.mult)
+                else:
+                    act(dst, src, 0.5)
+
+    g.wait_ge(T.sem.sent, 2 * R * n_eng)
+    for s in ("sv", "sa", "sp", "sg"):
+        g.wait_ge(T.sem[s], count[s])
+    g.wait_ge(T.sem.sto, stores[0])

@@ -5,13 +5,13 @@ R = 3
 PL = 1088
 BIG = 2.0 ** 99
 FAR = 2.0 ** 20
-SUMS = [(0, 0, 18), (7, 10, 16), (7, 10, 16)]
-PLAN = [("v", 0, 0, 256), ("a", 2, 0, 256), ("v", 1, 0, 256), ("a", 3, 0, 256), ("v", 0, 256, 512), ("a", 2, 256, 512), ("q", 0, 0, 256),
-        ("a", 3, 256, 512), ("a", 1, 256, 384), ("v", 1, 384, 512), ("q", 0, 256, 512)]
-LAST = [("v", 0, 0, 256), ("a", 2, 0, 256), ("v", 1, 0, 256), ("a", 3, 0, 256), ("q", 0, 0, 256),
-        ("a", 0, 256, 384), ("a", 1, 256, 384), ("v", 2, 256, 384), ("v", 3, 256, 384), ("y", "a", 0, 256), ("q", 1, 256, 384),
-        ("a", 0, 384, 512), ("v", 2, 384, 512), ("a", 1, 384, 512), ("v", 3, 384, 512), ("y", "a", 256, 384), ("q", 2, 384, 512), ("y", "v", 384, 512)]
-A_SPLIT = 8
+PLAN = [s for a in (0, 256) for s in (("v", 0, a, a + 256), ("a", 2, a, a + 256), ("v", 1, a, a + 256), ("a", 3, a, a + 256), ("q", 0, a, a + 256))]
+LAST = [s for a in (0, 128, 256, 384) for s in (("v", 0, a, a + 128), ("a", 2, a, a + 128), ("v", 1, a, a + 128), ("a", 3, a, a + 128),
+                                                ("q", a // 128, a, a + 128), ("y", "v" if a == 384 else "a", a, a + 128))]
+A_SPLIT = 4
+SUM_BY_LIST = 0
+FUSED = False
+EST = {"cyc": 1.0, "wake": 100.0, "gath": 1.56, "tt2": 1.0, "pe": 0.7, "dma": 1800.0, "bw": 280.0, "far": 2800.0, "first": 2000.0, "look": 0.25}
 
 
 def _sb(n, t):
@@ -31,7 +31,7 @@ SCRATCH = {
     "pen": _sb(96, F32), "gz": _sb(64, F32), "gd": _sb(32, F32), "ms": _sb(96, F32), "low": _sb(96, F32),
     "mx": _sb(8, F32), "l0": _sb(4, F32), "fl": _sb(24, F32), "zz": _sb(16, F32), "pr": _sb(16, F32), "dd": _sb(48, F32), "up": _sb(32, F32),
     "pb": _sb(128, BF), "tab": _sb(128, BF), "pg": _sb(512, BF), "pt": _sb(512, BF), "e2": _sb(320, BF), "en": _sb(160, F32),
-    "df": _sb(16, F32), "ht": _sb(32, F32), "ho": _sb(32, F32),
+    "df": _sb(16, F32), "ht": _sb(32, F32), "ho": _sb(32, F32), "c5": _sb(128, F32), "soff": _sb(128, U16),
 }
 for _r in range(R + 1):
     SCRATCH["xt%d" % _r] = _sb(2048, BF)
@@ -42,7 +42,40 @@ for _r in range(R):
 for _b in range(8):
     SCRATCH["ps%d" % _b] = ("psum", [128, 512], F32)
 
-SEMAPHORES = ["sv", "sa", "sp", "sg", "lx0", "lx1", "ll", "lu", "lw", "lv", "sto", "sent", "arr0", "arr1", "arr2"]
+SEMAPHORES = ["sv", "sa", "sp", "sg", "lx0", "lx1", "lh", "ld", "lu", "lw", "ls", "lv", "sto", "sent", "arr0", "arr1", "arr2"]
+ORDER = {}
+
+
+def schedule(ops):
+    n = len(ops)
+    after = [[] for _ in range(n)]
+    for i, o in enumerate(ops):
+        for j in o["deps"]:
+            after[j].append(i)
+    tail = [0.0] * n
+    for i in range(n - 1, -1, -1):
+        tail[i] = ops[i]["lat"] + max([tail[k] + (EST["wake"] if ops[k]["deps"][i] else 0.0) for k in after[i]] + [0.0])
+    left = [len(o["deps"]) for o in ops]
+    ready = {i: 0.0 for i in range(n) if left[i] == 0}
+    free, end, out = {}, [0.0] * n, []
+    while ready:
+        start = {i: max(t, free.get(ops[i]["q"], 0.0)) for i, t in ready.items()}
+        first = min(ready, key=lambda i: (start[i], -tail[i]))
+        q, t0 = ops[first]["q"], start[first]
+        best = max((i for i in ready if ops[i]["q"] == q and start[i] <= t0), key=lambda i: tail[i])
+        for i in ready:
+            if ops[i]["q"] == q and t0 < start[i] < t0 + EST["look"] * ops[best]["busy"] and tail[i] > tail[best] + ops[i]["busy"] + ops[best]["busy"]:
+                best = i
+        s = start[best]
+        free[q] = s + ops[best]["busy"]
+        end[best] = s + ops[best]["lat"]
+        out.append(best)
+        del ready[best]
+        for k in after[best]:
+            left[k] -= 1
+            if left[k] == 0:
+                ready[k] = max(end[j] + EST["wake"] if w else end[j] - ops[j]["lat"] for j, w in ops[k]["deps"].items())
+    return out
 
 
 def rank_program(g, core, T, topo):
@@ -55,119 +88,107 @@ def rank_program(g, core, T, topo):
     nxt = T.cores[(rank + 1) % n_ranks]
     eng = {"v": g.vector, "a": g.scalar, "p": g.tensor, "g": g, "s": g.sync}
     own = {"v": "sv", "a": "sa", "p": "sp", "g": "sg"}
-    count = {"sv": 0, "sa": 0, "sp": 0, "sg": 0}
-    known = {q: {} for q in eng}
-    hist = {}
+    ops, hist = [], {}
+    planned = "order" in ORDER
+    cyc = EST["cyc"]
 
     def v(name, a=0, b=None, s=1):
         if b is None:
             b = SCRATCH[name][1][1]
-        return (T[name][:, a:b:s] if s > 1 else T[name][:, a:b], [(name, frozenset(range(a, b, s)))])
+        return (T[name][:, a:b:s] if s > 1 else T[name][:, a:b], [(name, range(a, b, s))], len(range(a, b, s)), False, SCRATCH[name][2] == BF)
 
     def ind(win, off):
-        return (win[0].indirect(off[0]), win[1] + off[1])
+        return (win[0].indirect(off[0]), win[1] + off[1], 16 * off[2], True, win[4])
 
-    def wait(q, tok):
-        if known[q].get(tok[0], 0) < tok[1]:
-            eng[q].wait_ge(T.sem[tok[0]], tok[1])
-            known[q][tok[0]] = tok[1]
-        for s, n in tok[2].items():
-            if known[q].get(s, 0) < n:
-                known[q][s] = n
+    def add(q, fn, outs, ins, busy, lat=None, free=False, sem=None):
+        deps = {}
+        if not planned:
+            for views, w in ((ins, False), (outs, True)):
+                for name, el in [s for x in views for s in x[1]]:
+                    el = frozenset(el)
+                    for el2, w2, j in hist.get(name, []):
+                        if j == len(ops):
+                            continue
+                        if name.startswith("ps"):
+                            if ops[j]["q"] != q or ((w or w2) and not free):
+                                deps[j] = True
+                            elif w or w2:
+                                deps.setdefault(j, False)
+                        elif (w or w2) and not el.isdisjoint(el2):
+                            deps[j] = True
+                    hist.setdefault(name, []).append((el, w, len(ops)))
+        ops.append({"q": q, "fn": fn, "deps": deps, "busy": busy, "lat": busy if lat is None else lat, "sem": sem})
 
-    def order(q, reads, writes, free=False):
-        toks = []
-        for spans, w in ((reads, False), (writes, True)):
-            for name, el in spans:
-                for el2, w2, q2, tok in hist.get(name, []):
-                    if name.startswith("ps"):
-                        if q2 != q or ((w or w2) and not free):
-                            toks.append(tok)
-                    elif (w or w2) and not el.isdisjoint(el2):
-                        toks.append(tok)
-        for tok in sorted(toks, key=lambda t: -t[1]):
-            wait(q, tok)
+    def cost(o, ins, per):
+        if any(i[3] for i in ins):
+            return 55.0 + EST["gath"] * o[2] * cyc
+        return max(64.0, per * o[2]) * cyc
 
-    def note(q, reads, writes, tok):
-        for spans, w in ((reads, False), (writes, True)):
-            for name, el in spans:
-                hist.setdefault(name, []).append((el, w, q, tok))
+    queued = [EST["dma"]]
 
-    def op(q, fn, out, ins, free=False):
-        reads = [s for i in ins for s in i[1]]
-        writes = [s for o in out for s in o[1]]
-        order(q, reads, writes, free)
-        s = own[q]
-        fn().then_inc(T.sem[s], 1)
-        count[s] += 1
-        note(q, reads, writes, (s, count[s], dict(known[q])))
+    def load(q, out, in_, sem, nbytes, codes=False):
+        queued[0] += nbytes / EST["bw"]
+        add(q, lambda: eng[q].dma_start(out[0].bitcast(dt.uint8) if codes else out[0], in_), [out], [], 60.0, queued[0], sem=(sem, 16))
 
-    def load(q, out, in_, sem, total, codes=False):
-        eng[q].dma_start(out[0].bitcast(dt.uint8) if codes else out[0], in_).then_inc(T.sem[sem], 16)
-        note(sem, [], out[1], (sem, total, {}))
-
-    stores = [0]
-
-    def store(q, out, in_, view):
-        order(q, view[1], [])
-        eng[q].dma_start(out, in_).then_inc(T.sem.sto, 16)
-        stores[0] += 16
+    def store(q, out, in_, view, nbytes):
+        add(q, lambda: eng[q].dma_start(out, in_), [], [view], 60.0, EST["dma"] + nbytes / EST["bw"], sem=("sto", 16))
 
     def tt(o, a, b, alu):
-        op("v", lambda: g.vector.tensor_tensor(o[0], a[0], b[0], alu), [o], [a, b])
+        add("v", lambda: g.vector.tensor_tensor(o[0], a[0], b[0], alu), [o], [a, b], cost(o, [a], EST["tt2"] if o[4] and a[4] and b[4] else 2))
 
     def ts(o, a, s1, op0, s2=None, op1=None):
         ins = [a] + [s for s in (s1, s2) if isinstance(s, tuple)]
         x1 = s1[0] if isinstance(s1, tuple) else s1
         x2 = s2[0] if isinstance(s2, tuple) else s2
         if op1 is None:
-            op("v", lambda: g.vector.tensor_scalar(o[0], a[0], x1, None, op0), [o], ins)
+            add("v", lambda: g.vector.tensor_scalar(o[0], a[0], x1, None, op0), [o], ins, cost(o, [a], 1))
         else:
-            op("v", lambda: g.vector.tensor_scalar(o[0], a[0], x1, x2, op0, op1), [o], ins)
+            add("v", lambda: g.vector.tensor_scalar(o[0], a[0], x1, x2, op0, op1), [o], ins, cost(o, [a], 1))
 
     def cp(o, a):
-        op("v", lambda: g.vector.tensor_copy(o[0], a[0]), [o], [a])
+        add("v", lambda: g.vector.tensor_copy(o[0], a[0]), [o], [a], cost(o, [a], 1))
 
     def tr(o, a):
-        op("v", lambda: g.vector.transpose(o[0], a[0]), [o], [a])
+        add("v", lambda: g.vector.transpose(o[0], a[0]), [o], [a], cost(o, [a], 0.5 if o[4] else 1))
 
     def scan(o, d0, d1, op0, op1):
-        op("v", lambda: g.vector.tensor_tensor_scan(o[0], d0[0], d1[0], 0.0, op0, op1), [o], [d0, d1])
+        add("v", lambda: g.vector.tensor_tensor_scan(o[0], d0[0], d1[0], 0.0, op0, op1), [o], [d0, d1], cost(o, [], 1))
 
     def fill(o, c):
-        op("v", lambda: g.vector.memset(o[0], c), [o], [])
+        add("v", lambda: g.vector.memset(o[0], c), [o], [], cost(o, [], 0.5))
 
     def quant(c, s, t):
-        op("v", lambda: g.vector.quantize_mx(c[0], s[0], t[0]), [c, s], [t])
+        add("v", lambda: g.vector.quantize_mx(c[0], s[0], t[0]), [c, s], [t], (12 + 0.22 * t[2]) * cyc / 0.83)
 
     def act(o, a, scale=None, bias=None):
         if bias is not None:
-            op("a", lambda: g.scalar.activation(o[0], a[0], ACT.Identity, bias=bias, scale=scale), [o], [a])
+            add("a", lambda: g.scalar.activation(o[0], a[0], ACT.Identity, bias=bias, scale=scale), [o], [a], cost(o, [a], 1))
         elif scale is None:
-            op("a", lambda: g.scalar.activation(o[0], a[0], ACT.Copy), [o], [a])
+            add("a", lambda: g.scalar.activation(o[0], a[0], ACT.Copy), [o], [a], cost(o, [a], 1))
         else:
-            op("a", lambda: g.scalar.activation(o[0], a[0], ACT.Copy, scale=scale), [o], [a])
+            add("a", lambda: g.scalar.activation(o[0], a[0], ACT.Copy, scale=scale), [o], [a], cost(o, [a], 1))
 
     def mm(o, lq, ls, rq, rs, start=True, stop=True):
-        op("p", lambda: g.tensor.matmul_mx(o[0], lq[0], ls[0], rq[0], rs[0], start, stop), [o], [lq, ls, rq, rs], free=not start)
+        add("p", lambda: g.tensor.matmul_mx(o[0], lq[0], ls[0], rq[0], rs[0], start, stop), [o], [lq, ls, rq, rs], (o[2] + 16) * EST["pe"], free=not start)
 
     def iota(o, pattern, base, cm, flt=True):
         if flt:
-            op("g", lambda: g.iota(o[0], pattern, base, cm, allow_small_or_imprecise_dtypes=True), [o], [])
+            add("g", lambda: g.iota(o[0], pattern, base, cm, allow_small_or_imprecise_dtypes=True), [o], [], 130 + 2 * o[2] * cyc)
         else:
-            op("g", lambda: g.iota(o[0], pattern, base, cm), [o], [])
+            add("g", lambda: g.iota(o[0], pattern, base, cm), [o], [], 130 + 2 * o[2] * cyc)
 
     def bytes_of(view):
         return view[0].bitcast(dt.uint8)
 
-    load("a", v("src", 32, 44), T.hg[:, :], "ll", 32)
-    load("s", v("xt0", 0, 1024), T.x[:, 0:1024], "lx0", 16)
-    load("a", v("src", 0, 32), T.dg[:, :], "ll", 32)
-    load("s", v("xt0", 1024, 2048), T.x[:, 1024:2048], "lx1", 16)
-    load("a", v("ub"), T.u[:, :], "lu", 16)
-    load("s", v("wq"), T.wc[:, :], "lw", 32, codes=True)
-    load("s", v("wp"), T.ws[:, :], "lw", 32)
-    load("s", v("vb"), T.v[:, :], "lv", 16)
+    load("a", v("src", 32, 44), T.hg[:, :], "lh", 6144)
+    load("a", v("src", 0, 32), T.dg[:, :], "ld", 16384)
+    load("s", v("xt0", 0, 1024), T.x[:, 0:1024], "lx0", 262144)
+    load("a", v("ub"), T.u[:, :], "lu", 131072)
+    load("s", v("xt0", 1024, 2048), T.x[:, 1024:2048], "lx1", 262144)
+    load("s", v("wq"), T.wc[:, :], "lw", 262144, codes=True)
+    load("s", v("wp"), T.ws[:, :], "ls", 65536)
+    load("s", v("vb"), T.v[:, :], "lv", 131072)
+    n_loads = len(ops)
 
     fill(v("ec"), 64.0)
     iota(v("pi"), [[0, 1]], 0, 1, flt=False)
@@ -179,19 +200,20 @@ def rank_program(g, core, T, topo):
     iota(v("cc", 16, 20), [[1, 2], [2, 2]], 36, 0)
     iota(v("c6"), [[1024, 2], [0, 8], [1, 4]], 28, 0)
     iota(v("y4"), [[0, 4], [1, 4], [0, 4]], 0, 0)
-    op("g", lambda: g.affine_select(v("eb")[0], v("ec")[0], [[-1, 528]], A.is_equal, 0.0, 3, 4), [v("eb")], [v("ec")])
+    add("g", lambda: g.affine_select(v("eb")[0], v("ec")[0], [[-1, 528]], A.is_equal, 0.0, 3, 4), [v("eb")], [v("ec")], 170 + 1056 * cyc)
     act(v("sf", 44, 64), v("ec", 0, 20), 0.0)
     act(v("at", 256, 512), v("ec", 0, 256), 0.0)
     act(v("gt", 256, 512), v("ec", 0, 256), 0.0)
     act(v("pb"), v("ec", 0, 128), 0.0)
     act(v("ht"), v("ec", 0, 32), 0.0)
     act(v("zs"), v("ec", 0, 64), 0.0)
-    for r in range(R):
-        act(v("xh%d" % r, 1, 4 * PL, 16), v("ec", 0, 4 * PL // 16), 0.0)
+    if not SUM_BY_LIST:
+        for r in range(R):
+            act(v("xh%d" % r, 1, 4 * PL, 16), v("ec", 0, 4 * PL // 16), 0.0)
     for i, m in enumerate((7, 8, 4, 6, 31, 1, 3)):
         ts(v("bi", i, i + 1), v("pi"), m, A.bitwise_and)
     cp(v("bf", 0, 7), v("bi", 0, 7))
-    b7, b8, b4, b6, b31, b1, b3, x0, x1, x2, x3, x4 = (v("bf", i, i + 1) for i in range(12))
+    b7, b8, b4, b6, b31, b1, b3, x0, x1, x2, x3, x4, x5 = (v("bf", i, i + 1) for i in range(13))
     CL, BL, AL, ML, CD, DL, GL, NL = (v("off", a, b) for a, b in ((0, 4), (4, 6), (6, 8), (8, 14), (14, 15), (16, 19), (20, 24), (24, 28)))
     ts(v("rst"), v("kk"), 8.0, A.is_equal, BIG, A.mult)
     ts(x0, b7, 16.0, A.mult, b8, A.add)
@@ -216,6 +238,10 @@ def rank_program(g, core, T, topo):
     ts(v("m1"), v("c6"), 0.25, A.mult, x2, A.add)
     ts(v("m2"), v("y4"), b3, A.not_equal, -FAR, A.mult)
     tt(v("mb"), v("m1"), v("m2"), A.add)
+    if SUM_BY_LIST:
+        iota(v("c5"), [[1, 4], [8, 32]], 0, 0)
+        ts(x5, b8, 0.5, A.mult)
+        ts(v("soff"), v("c5"), x5, A.add)
 
     PF, PM, HC, SX = (v("st", 32 * i, 32 * i + 32) for i in range(4))
     D = v("src", 0, 32)
@@ -237,86 +263,83 @@ def rank_program(g, core, T, topo):
     quant(v("uq"), v("us"), v("ub"))
     for par in range(2):
         o = "o%d" % par
-        ts(v("zz", 4 * par, 4 * par + 4, 2), v(o, 16, 18), -1.0, A.mult, 8.0, A.add)
-        cp(v("zz", 4 * par + 1, 4 * par + 4, 2), v(o, 20, 22))
+        for c in (0, 8):
+            act(v("zz", c + 4 * par, c + 4 * par + 4, 2), v(o, 16, 18), -1.0, 8.0)
+            act(v("zz", c + 4 * par + 1, c + 4 * par + 4, 2), v(o, 20, 22))
+        ts(v("loff", par, 32, 2), v(o, 0, 16), 64.0 * par, A.add)
     quant(v("xq", 0, 256), v("xs", 0, 256), v("xt0", 0, 1024))
-    cp(v("zz", 8, 16), v("zz", 0, 8))
     quant(v("xq", 256, 512), v("xs", 256, 512), v("xt0", 1024, 2048))
-
-    def entry_tables():
-        ts(v("si", 64, 96), D, 3, A.logical_shift_right, 31, A.bitwise_and)
-        ts(SX, D, 256.0, A.is_ge, 0.5, A.mult)
-        ts(HC, v("si", 64, 96), 512.0, A.add)
-        quant(v("vq"), v("vs"), v("vb"))
-        tt(HC, HC, SX, A.add)
-
-    def penalties():
-        tt(v("gz"), ind(v("zz", 0, 8), GL), v("kk", 0, 64), A.is_ge)
-        ts(v("pen", 0, 32), v("gz", 0, 32), BIG, A.mult)
-        tt(v("gd"), v("gz", 32, 64), v("gz", 0, 32), A.is_ge)
-        ts(v("pen", 64, 96), v("gz", 32, 64), -BIG, A.mult, BIG, A.add)
-        ts(v("pen", 32, 64), v("gd"), BIG, A.mult)
-
-    def doubles(r, t):
-        act(v("xh%d" % r, PL * t, PL * t + 1024, 2), v("xt%d" % r, t, 2048, 4), 2.0)
+    ts(v("si", 64, 96), D, 3, A.logical_shift_right, 31, A.bitwise_and)
+    ts(SX, D, 256.0, A.is_ge, 0.5, A.mult)
+    ts(HC, v("si", 64, 96), 512.0, A.add)
+    tt(HC, HC, SX, A.add)
+    quant(v("vq"), v("vs"), v("vb"))
+    for b in range(4):
+        quant(v("eq", 128 * b, 128 * b + 128), v("es", 128 * b, 128 * b + 128), v("eb", 3 - b, 515 - b))
 
     n_eng = min(len(topo.engines(T.cores[i], T.cores[(i + 1) % n_ranks])) for i in range(n_ranks))
     mask = sum(1 << e for e in topo.engines(core, nxt)[:n_eng])
     rid, pid, _se = topo.addr(nxt)
 
+    def sender(r):
+        cq, cs = "cq%d" % r, "cs%d" % r
+
+        def fn():
+            g.remote_dma(bytes_of(v(cq, 0, 64)), bytes_of(v(cq, 64, 128)), T.sem["arr%d" % r], T.sem.sent, pid, rid, mask)
+            g.remote_dma(v(cs, 0, 64)[0], v(cs, 64, 128)[0], T.sem["arr%d" % r], T.sem.sent, pid, rid, mask)
+        add("g", fn, [v(cq, 0, 64), v(cs, 0, 64)], [v(cq, 64, 128), v(cs, 64, 128)], 600.0, EST["far"] + (EST["first"] if r == 0 else 0.0),
+            sem=("arr%d" % r, 2 * n_eng))
+
     for r in range(R):
         xt, xh, cq, cs, xn = "xt%d" % r, "xh%d" % r, "cq%d" % r, "cs%d" % r, "xt%d" % (r + 1)
         mm(v("ps0"), v("uq"), v("us"), v("xq"), v("xs"))
-        penalties()
-        for t in range(3 if r == 0 else 4):
-            doubles(r, t)
+        tt(v("gz"), ind(v("zz", 0, 8), GL), v("kk", 0, 64), A.is_ge)
+        ts(v("pen", 0, 32), v("gz", 0, 32), BIG, A.mult)
+        tt(v("gd"), v("gz", 32, 64), v("gz", 0, 32), A.is_ge)
+        ts(v("pen", 64, 96), v("gz", 32, 64), -BIG, A.mult, BIG, A.add)
+        ts(v("pen", 32, 64), v("gd"), BIG, A.mult)
+        for t in range(4):
+            for h in range(2):
+                act(v(xh, PL * t + 512 * h, PL * t + 512 * h + 512, 2), v(xt, 1024 * h + t, 1024 * h + 1024, 4), 2.0)
         for k in range(8):
             tr(v("tt", 64 * k, 64 * k + 64), v("ps0", k, 512, 8))
         cp(v("sc"), ind(v("tt"), CL))
         scan(v("pm"), v("rst", 0, 64), v("sc"), A.add, A.min)
-        tt(v("ms"), ind(v("sc", 0, 32), ML), v("pen"), A.add)
         tt(v("ge"), ind(v("pm", 0, 32), BL), v("pm", 32, 64), A.is_ge)
-        scan(v("low"), v("rst"), v("ms"), A.add, A.min)
         scan(v("wb", 0, 32), v("rm"), v("ge"), A.mult, A.add)
-        tt(v("mx"), v("low", 7, 64, 8), v("low", 39, 96, 8), A.max)
         tt(v("a1"), ind(v("wb", 0, 32), AL), v("ab"), A.subtract)
-        tt(v("fl", 0, 16), ind(v("wb", 0, 32), CD), v("zz"), A.is_gt)
         tr(v("a2"), v("a1"))
-        tt(v("l0"), v("low", 7, 32, 8), v("mx", 4, 8), A.is_ge)
         tt(v("a3"), v("a2", 0, 32, 2), v("a2", 1, 32, 2), A.min)
-        tt(v("fl", 17, 24, 2), v("mx", 0, 4), v("low", 71, 96, 8), A.is_ge)
         ts(v("aoff"), v("a3"), -4.0, A.mult)
         if A_SPLIT < 16:
             act(v("at", 16 * A_SPLIT, 256), ind(v(xt), v("aoff", A_SPLIT, 16)))
-        tt(v("fl", 16, 24, 2), v("l0"), v("fl", 8, 16, 2), A.is_gt)
         if A_SPLIT:
             cp(v("at", 0, 16 * A_SPLIT), ind(v(xt), v("aoff", 0, A_SPLIT)))
-        tt(v("pr"), v("fl", 8, 24), v("zz"), A.mult)
-        if A_SPLIT < 8:
-            tt(v("wb", 40, 44), v("mx", 0, 4), v("mx", 4, 8), A.max)
-            tt(v("wb", 32, 40), v("pr", 0, 16, 2), v("pr", 1, 16, 2), A.max)
-            tt(v("df", 0, 8), v("fl", 8, 16), v("fl", 16, 24), A.subtract)
         quant(v(cq, 64, 192), v(cs, 64, 192), v("at"))
-        order("g", v(cq, 64, 128)[1] + v(cs, 64, 128)[1], [])
-        g.remote_dma(bytes_of(v(cq, 0, 64)), bytes_of(v(cq, 64, 128)), T.sem["arr%d" % r], T.sem.sent, pid, rid, mask)
-        g.remote_dma(v(cs, 0, 64)[0], v(cs, 64, 128)[0], T.sem["arr%d" % r], T.sem.sent, pid, rid, mask)
-        note("far", [], v(cq, 0, 64)[1] + v(cs, 0, 64)[1], ("arr%d" % r, 2 * n_eng, {}))
-        if A_SPLIT >= 8:
-            tt(v("wb", 32, 40), v("pr", 0, 16, 2), v("pr", 1, 16, 2), A.max)
-            tt(v("wb", 40, 44), v("mx", 0, 4), v("mx", 4, 8), A.max)
+        sender(r)
+        tt(v("ms"), ind(v("sc", 0, 32), ML), v("pen"), A.add)
+        scan(v("low"), v("rst"), v("ms"), A.add, A.min)
+        tt(v("mx"), v("low", 7, 64, 8), v("low", 39, 96, 8), A.max)
+        tt(v("fl", 0, 16), ind(v("wb", 0, 32), CD), v("zz"), A.is_gt)
+        tt(v("l0"), v("low", 7, 32, 8), v("mx", 4, 8), A.is_ge)
+        tt(v("fl", 17, 24, 2), v("mx", 0, 4), v("low", 71, 96, 8), A.is_ge)
+        tt(v("fl", 16, 24, 2), v("l0"), v("fl", 8, 16, 2), A.is_gt)
+        tt(v("pr"), v("fl", 8, 24), v("zz"), A.mult)
+        tt(v("wb", 32, 40), v("pr", 0, 16, 2), v("pr", 1, 16, 2), A.max)
+        tt(v("wb", 40, 44), v("mx", 0, 4), v("mx", 4, 8), A.max)
         tt(v("m1"), ind(v("wb", 0, 44), NL), v("mb"), A.subtract)
         cp(v("dd"), ind(v("wb", 0, 44), DL))
         ZA, ZL, C1, C, MM = (v("dd", 8 * i, 8 * i + 8) for i in range(5))
         B0, B1, HP, T2, BS, NN = (v("pb", i, 128, 16) for i in (0, 4, 8, 12, 1, 9))
         UP, NU, FL, BZ = (v("up", 8 * i, 8 * i + 8) for i in range(4))
         tr(v("m2"), v("m1"))
-        tt(NN, C1, ZA, A.subtract)
         tt(v("m3", 0, 32), v("m2", 0, 64, 2), v("m2", 1, 64, 2), A.min)
-        tt(UP, ZL, C, A.is_lt)
         tt(v("m3", 32, 48), v("m3", 0, 32, 2), v("m3", 1, 32, 2), A.min)
-        tt(NU, NN, UP, A.mult)
         ts(v("moff"), v("m3", 32, 48), -4.0, A.mult, 0.0, A.max)
         act(v("mg"), ind(v(xt), v("moff")))
+        tt(NN, C1, ZA, A.subtract)
+        tt(UP, ZL, C, A.is_lt)
+        tt(NU, NN, UP, A.mult)
         ts(FL, MM, BIG / 2, A.is_lt, 0.5, A.mult)
         tt(B0, ZL, NU, A.add)
         tt(BZ, FL, ZA, A.subtract)
@@ -324,40 +347,29 @@ def rank_program(g, core, T, topo):
         tt(HP, ZA, NU, A.add)
         tt(T2, B1, NU, A.add)
         tt(BS, BZ, B0, A.subtract)
-        if A_SPLIT >= 8:
-            tt(v("df", 0, 8), v("fl", 8, 16), v("fl", 16, 24), A.subtract)
+        tt(v("df", 0, 8), v("fl", 8, 16), v("fl", 16, 24), A.subtract)
         tr(v("tab"), v("pb"))
-        if r == 0:
-            for par in range(2):
-                ts(v("loff", par, 32, 2), v("o%d" % par, 0, 16), 64.0 * par, A.add)
         act(v("pg", 0, 256), ind(v("tab"), v("loff", 0, 16)))
         act(v("pg", 256, 512), ind(v("tab"), v("loff", 16, 32)))
-        if r == 0:
-            doubles(0, 3)
-            for b in range(4):
-                quant(v("eq", 128 * b, 128 * b + 128), v("es", 128 * b, 128 * b + 128), v("eb", 3 - b, 515 - b))
-            entry_tables()
         for b in range(8):
             e = b % 4
             mm(v("ps%d" % b, 0, 128), v("eq", 128 * e, 128 * e + 128), v("es", 128 * e, 128 * e + 128), v(cq, 0, 128), v(cs, 0, 128), True, b < 4)
         for b in range(4):
             act(v("gt", b, 256, 4), v("ps%d" % b, 0, 64), 2.0 ** -6)
-        done = [0]
-
-        def sums(upto):
-            while done[0] < upto:
-                t, k = divmod(done[0], 7)
-                tt(v(xh, PL * t + 2 * k + 3, PL * t + 1024, 16), v(xt, 4 * k + 4 + t, 2048, 32), v("mg", t, 256, 4), A.add)
-                done[0] += 1
+        for t in range(4):
+            if SUM_BY_LIST:
+                for a in range(0, 512, SUM_BY_LIST):
+                    b = a + SUM_BY_LIST
+                    tt(v(xh, PL * t + 2 * a + 1, PL * t + 2 * b, 2), ind(v("mg"), v("soff", 32 * t + a // 16, 32 * t + b // 16)), v(xt, 4 * a + t, 4 * b, 4), A.add)
+            else:
+                for k in range(1, 8):
+                    tt(v(xh, PL * t + 2 * k + 1, PL * t + 1024, 16), v(xt, 4 * k + t, 2048, 32), v("mg", t, 256, 4), A.add)
         tt(v("df", 8, 16), v("df", 0, 8), NN, A.mult)
-        sums(SUMS[r][0])
-        tr(v("pt", 0, 256), v("pg", 0, 256))
         tt(v("zz", 0, 8), v("zz", 0, 8), v("df", 8, 16), A.add)
         if r < R - 1:
-            tt(v("zz", 8, 16), v("zz", 8, 16), v("df", 8, 16), A.add)
-        sums(SUMS[r][1])
+            act(v("zz", 8, 16), v("zz", 0, 8))
+        tr(v("pt", 0, 256), v("pg", 0, 256))
         tr(v("pt", 256, 512), v("pg", 256, 512))
-        sums(done[0] + 1)
         tt(v("e2", 0, 128), v("pt", 0, 512, 4), v("p4"), A.is_ge)
         tt(v("e2", 192, 256), v("pt", 1, 512, 8), v("zs"), A.add)
         tt(v("e2", 128, 192), v("e2", 0, 128, 2), v("e2", 1, 128, 2), A.subtract)
@@ -365,13 +377,9 @@ def rank_program(g, core, T, topo):
         tt(v("e2", 256, 320), v("e2", 128, 192), v("e2", 192, 256), A.mult)
         tt(v("en", 32, 64), v("en", 0, 32), HC, A.mult)
         tt(v("en", 64, 96), v("e2", 256, 320, 2), v("e2", 257, 320, 2), A.add)
-        sums(done[0] + 1)
         tt(v("en", 96, 128), v("en", 64, 96), D, A.add)
-        sums(done[0] + 1)
         tt(v("en", 128, 160), v("en", 96, 128), v("en", 32, 64), A.max)
-        sums(done[0] + 1)
         ts(v("em16"), v("en", 128, 160), 2.0, A.mult)
-        sums(SUMS[r][2])
         quant(v("gq"), v("gs"), v("gt"))
         for b in range(4):
             mm(v("ps%d" % (4 + b), 0, 128), v("wq", 128 * b, 128 * b + 128), v("wp", 128 * b, 128 * b + 128), v("gq"), v("gs"), False, True)
@@ -380,14 +388,12 @@ def rank_program(g, core, T, topo):
         if r == R - 1:
             for h in range(2):
                 z0, z1 = v("zz", 2 * h, 8, 4), v("zz", 2 * h + 1, 8, 4)
-                ts(v("ht", h, 12, 6), z0, -1.0, A.mult, 8.0, A.add)
+                act(v("ht", h, 12, 6), z0, -1.0, 8.0)
                 tt(v("ht", 2 + h, 12, 6), z0, z1, A.subtract)
-                cp(v("ht", 4 + h, 12, 6), z1)
-            sums(done[0] + 1)
+                act(v("ht", 4 + h, 12, 6), z1)
             tr(v("ho"), v("ht"))
             for a in range(4):
-                store("s", T.oh[2 * a:2 * a + 2, :], T.ho[32 * a:32 * a + 12, :], v("ho"))
-        sums(28)
+                store("s", T.oh[2 * a:2 * a + 2, :], T.ho[32 * a:32 * a + 12, :], v("ho"), 1536)
         bank = {}
         for kind, t, a, b in (PLAN if r < R - 1 else LAST):
             if kind == "q":
@@ -395,13 +401,13 @@ def rank_program(g, core, T, topo):
                 if r == R - 1:
                     bank[a] = "ps%d" % t
                     mm(v(bank[a], 0, b - a), v("vq"), v("vs"), v("xq", a, b), v("xs", a, b))
-                    store("s", T.oc[:, 4 * a:4 * b], bytes_of(v("xq", a, b)), v("xq", a, b))
+                    store("s", T.oc[:, 4 * a:4 * b], bytes_of(v("xq", a, b)), v("xq", a, b), 1024 * (512 - a))
                     if b == 512:
                         for k in range(4):
-                            store("s", T.osc[4 * k:4 * k + 4, :], T.xs[32 * k:32 * k + 4, :], v("xs"))
+                            store("s", T.osc[4 * k:4 * k + 4, :], T.xs[32 * k:32 * k + 4, :], v("xs"), 2048)
             elif kind == "y":
                 (cp if t == "v" else act)(v("yb", a, b), v(bank[a], 0, b - a))
-                store("a", T.y[:, a:b], v("yb", a, b)[0], v("yb", a, b))
+                store("a", T.y[:, a:b], v("yb", a, b)[0], v("yb", a, b), 1024 * (512 - a) - 512 * (b - a))
             else:
                 src = ind(v(xh, PL * t, PL * t + PL), v("em16", a // 16, b // 16))
                 dst = v(xn, 4 * a + t, 4 * b, 4)
@@ -410,7 +416,39 @@ def rank_program(g, core, T, topo):
                 else:
                     act(dst, src, 0.5)
 
+    if not planned:
+        for i in range(1, n_loads):
+            prev = [j for j in range(i) if ops[j]["q"] == ops[i]["q"]]
+            if prev:
+                ops[i]["deps"][prev[-1]] = False
+        ORDER["order"] = schedule(ops)
+        ORDER["deps"] = [o["deps"] for o in ops]
+    count = {"sv": 0, "sa": 0, "sp": 0, "sg": 0, "sto": 0}
+    known = {q: {} for q in eng}
+    token = {}
+    for i in ORDER["order"]:
+        o = ops[i]
+        q = o["q"]
+        for tok in sorted((token[j] for j, w in ORDER["deps"][i].items() if w), key=lambda t: -t[1]):
+            if known[q].get(tok[0], 0) < tok[1]:
+                eng[q].wait_ge(T.sem[tok[0]], tok[1])
+                known[q][tok[0]] = tok[1]
+            for s, n in tok[2].items():
+                if known[q].get(s, 0) < n:
+                    known[q][s] = n
+        if o["sem"] is None:
+            s = own[q]
+            o["fn"]().then_inc(T.sem[s], 1)
+            count[s] += 1
+            token[i] = (s, count[s], dict(known[q]))
+        elif q == "g":
+            o["fn"]()
+            token[i] = (o["sem"][0], o["sem"][1], {})
+        else:
+            o["fn"]().then_inc(T.sem[o["sem"][0]], 16)
+            if o["sem"][0] == "sto":
+                count["sto"] += 16
+            token[i] = (o["sem"][0], 16, {})
     g.wait_ge(T.sem.sent, 2 * R * n_eng)
-    for s in ("sv", "sa", "sp", "sg"):
+    for s in count:
         g.wait_ge(T.sem[s], count[s])
-    g.wait_ge(T.sem.sto, stores[0])

@@ -8,10 +8,8 @@ FAR = 2.0 ** 20
 PLAN = [s for a in (0, 256) for s in (("v", 0, a, a + 256), ("a", 2, a, a + 256), ("v", 1, a, a + 256), ("a", 3, a, a + 256), ("q", 0, a, a + 256))]
 LAST = [s for a in (0, 128, 256, 384) for s in (("v", 0, a, a + 128), ("a", 2, a, a + 128), ("v", 1, a, a + 128), ("a", 3, a, a + 128),
                                                 ("q", a // 128, a, a + 128), ("y", "v" if a == 384 else "a", a, a + 128))]
-A_SPLIT = 4
-SUM_BY_LIST = 0
-FUSED = False
-EST = {"cyc": 1.0, "wake": 100.0, "gath": 1.56, "tt2": 1.0, "pe": 0.7, "dma": 1800.0, "bw": 280.0, "far": 2800.0, "first": 2000.0, "look": 0.25}
+A_SPLIT = 6
+EST = {"cyc": 1.0, "wake": 100.0, "gath": 1.56, "tt2": 1.0, "pe": 0.7, "dma": 1800.0, "bw": 280.0, "far": 2800.0, "first": 2000.0}
 
 
 def _sb(n, t):
@@ -26,12 +24,12 @@ SCRATCH = {
     "src": _sb(48, I32), "si": _sb(96, I32), "sf": _sb(64, F32), "ta": _sb(48, F32), "tb": _sb(48, F32), "o0": _sb(32, F32), "o1": _sb(32, F32),
     "pi": _sb(1, I32), "bi": _sb(8, I32), "bf": _sb(16, F32), "cc": _sb(24, F32), "kk": _sb(96, F32), "rst": _sb(96, F32), "rm": _sb(32, F32),
     "c4": _sb(32, F32), "yp": _sb(32, F32), "ab": _sb(32, F32), "off": _sb(32, U16), "loff": _sb(32, U16), "aoff": _sb(16, U16), "em16": _sb(32, U16),
-    "st": _sb(128, F32), "p4": _sb(128, BF), "zs": _sb(64, BF), "tt": _sb(512, F32), "sc": _sb(64, F32), "pm": _sb(64, F32), "ge": _sb(32, F32), "wb": _sb(48, F32),
+    "st": _sb(128, F32), "p4": _sb(128, BF), "zs": _sb(64, BF), "tt": _sb(512, F32), "pm": _sb(64, F32), "ge": _sb(32, F32), "wb": _sb(48, F32),
     "a1": _sb(32, F32), "a2": _sb(32, F32), "a3": _sb(16, F32), "m1": _sb(64, F32), "m2": _sb(64, F32), "m3": _sb(48, F32),
     "pen": _sb(96, F32), "gz": _sb(64, F32), "gd": _sb(32, F32), "ms": _sb(96, F32), "low": _sb(96, F32),
     "mx": _sb(8, F32), "l0": _sb(4, F32), "fl": _sb(24, F32), "zz": _sb(16, F32), "pr": _sb(16, F32), "dd": _sb(48, F32), "up": _sb(32, F32),
     "pb": _sb(128, BF), "tab": _sb(128, BF), "pg": _sb(512, BF), "pt": _sb(512, BF), "e2": _sb(320, BF), "en": _sb(160, F32),
-    "df": _sb(16, F32), "ht": _sb(32, F32), "ho": _sb(32, F32), "c5": _sb(128, F32), "soff": _sb(128, U16),
+    "df": _sb(16, F32), "ht": _sb(32, F32), "ho": _sb(32, F32), "u2": _sb(128, CODE), "s2": _sb(128, U8), "uoff": _sb(8, U16), "cu": _sb(8, F32),
 }
 for _r in range(R + 1):
     SCRATCH["xt%d" % _r] = _sb(2048, BF)
@@ -63,9 +61,6 @@ def schedule(ops):
         first = min(ready, key=lambda i: (start[i], -tail[i]))
         q, t0 = ops[first]["q"], start[first]
         best = max((i for i in ready if ops[i]["q"] == q and start[i] <= t0), key=lambda i: tail[i])
-        for i in ready:
-            if ops[i]["q"] == q and t0 < start[i] < t0 + EST["look"] * ops[best]["busy"] and tail[i] > tail[best] + ops[i]["busy"] + ops[best]["busy"]:
-                best = i
         s = start[best]
         free[q] = s + ops[best]["busy"]
         end[best] = s + ops[best]["lat"]
@@ -197,7 +192,8 @@ def rank_program(g, core, T, topo):
     iota(v("kk"), [[0, 12], [-1, 8]], 8, 0)
     iota(v("c4"), [[0, 4], [1024, 2], [1, 4]], 32, 0)
     iota(v("yp"), [[0, 2], [1, 2], [0, 8]], 0, 0)
-    iota(v("cc", 16, 20), [[1, 2], [2, 2]], 36, 0)
+    iota(v("cc", 16, 20), [[1, 4]], 36, 0)
+    iota(v("cu"), [[2, 4], [0, 2]], 0, 0)
     iota(v("c6"), [[1024, 2], [0, 8], [1, 4]], 28, 0)
     iota(v("y4"), [[0, 4], [1, 4], [0, 4]], 0, 0)
     add("g", lambda: g.affine_select(v("eb")[0], v("ec")[0], [[-1, 528]], A.is_equal, 0.0, 3, 4), [v("eb")], [v("ec")], 170 + 1056 * cyc)
@@ -207,24 +203,22 @@ def rank_program(g, core, T, topo):
     act(v("pb"), v("ec", 0, 128), 0.0)
     act(v("ht"), v("ec", 0, 32), 0.0)
     act(v("zs"), v("ec", 0, 64), 0.0)
-    if not SUM_BY_LIST:
-        for r in range(R):
-            act(v("xh%d" % r, 1, 4 * PL, 16), v("ec", 0, 4 * PL // 16), 0.0)
+    for r in range(R):
+        act(v("xh%d" % r, 1, 4 * PL, 16), v("ec", 0, 4 * PL // 16), 0.0)
     for i, m in enumerate((7, 8, 4, 6, 31, 1, 3)):
         ts(v("bi", i, i + 1), v("pi"), m, A.bitwise_and)
     cp(v("bf", 0, 7), v("bi", 0, 7))
-    b7, b8, b4, b6, b31, b1, b3, x0, x1, x2, x3, x4, x5 = (v("bf", i, i + 1) for i in range(13))
-    CL, BL, AL, ML, CD, DL, GL, NL = (v("off", a, b) for a, b in ((0, 4), (4, 6), (6, 8), (8, 14), (14, 15), (16, 19), (20, 24), (24, 28)))
+    b7, b8, b4, b6, b31, b1, b3, x0, x1, x2, x3, x4 = (v("bf", i, i + 1) for i in range(12))
+    BL, AL, ML, CD, DL, GL, NL = (v("off", a, b) for a, b in ((4, 6), (6, 8), (8, 14), (14, 15), (16, 19), (20, 24), (24, 28)))
     ts(v("rst"), v("kk"), 8.0, A.is_equal, BIG, A.mult)
-    ts(x0, b7, 16.0, A.mult, b8, A.add)
-    ts(x1, b4, 2.0, A.mult, 7.0, A.add)
+    ts(x1, b4, 8.0, A.mult, 14.0, A.add)
     ts(x2, b31, 8.0, A.mult)
     ts(x3, b8, 0.5, A.mult, 32.0, A.add)
     ts(x4, b8, 0.125, A.mult, 6.0, A.add)
     ts(v("rm"), v("kk", 0, 32), 8.0, A.not_equal)
-    ts(CL, v("cc", 6, 14, 2), x0, A.add, 4.0, A.mult)
+    ts(v("uoff"), v("cu"), b1, A.add, 16.0, A.mult)
     ts(BL, v("cc", 0, 2), b8, A.add, 7.0, A.add)
-    ts(AL, v("cc", 0, 2), x1, A.add)
+    ts(AL, v("cc", 0, 2), x1, A.add, 0.5, A.mult)
     ts(v("a1"), v("c4"), 0.25, A.mult, x2, A.add)
     ts(v("a2"), v("yp"), b1, A.not_equal, -FAR, A.mult)
     ts(GL, v("cc", 6, 10), b8, A.add, 0.25, A.mult)
@@ -238,17 +232,14 @@ def rank_program(g, core, T, topo):
     ts(v("m1"), v("c6"), 0.25, A.mult, x2, A.add)
     ts(v("m2"), v("y4"), b3, A.not_equal, -FAR, A.mult)
     tt(v("mb"), v("m1"), v("m2"), A.add)
-    if SUM_BY_LIST:
-        iota(v("c5"), [[1, 4], [8, 32]], 0, 0)
-        ts(x5, b8, 0.5, A.mult)
-        ts(v("soff"), v("c5"), x5, A.add)
 
     PF, PM, HC, SX = (v("st", 32 * i, 32 * i + 32) for i in range(4))
     D = v("src", 0, 32)
     ts(v("si", 0, 32), D, 3, A.logical_shift_right)
     cp(v("sf", 32, 44), v("src", 32, 44))
     ts(v("si", 32, 64), D, 7, A.bitwise_and)
-    cp(v("sf", 0, 32), v("si", 0, 32))
+    ts(v("m3", 0, 32), D, 256.0, A.is_ge, 32.0, A.mult)
+    tt(v("sf", 0, 32), v("si", 0, 32), v("m3", 0, 32), A.add)
     cp(PF, v("si", 32, 64))
     tr(v("tb", 0, 32), v("sf", 0, 64, 2))
     tr(v("ta", 16, 48), v("sf", 1, 64, 2))
@@ -261,12 +252,14 @@ def rank_program(g, core, T, topo):
     tr(v("o0"), v("ta", 0, 32))
     tr(v("o1"), v("tb", 16, 48))
     quant(v("uq"), v("us"), v("ub"))
+    add("v", lambda: g.vector.tensor_copy(v("u2")[0].bitcast(dt.uint32), v("uq")[0].bitcast(dt.uint32).indirect(v("uoff")[0])), [v("u2")], [v("uq"), v("uoff")], 255.0)
+    act(v("s2"), ind(v("us"), v("uoff")))
     for par in range(2):
         o = "o%d" % par
         for c in (0, 8):
-            act(v("zz", c + 4 * par, c + 4 * par + 4, 2), v(o, 16, 18), -1.0, 8.0)
-            act(v("zz", c + 4 * par + 1, c + 4 * par + 4, 2), v(o, 20, 22))
-        ts(v("loff", par, 32, 2), v(o, 0, 16), 64.0 * par, A.add)
+            act(v("zz", c + 2 * par, c + 8, 4), v(o, 16, 18), -1.0, 8.0)
+            act(v("zz", c + 2 * par + 1, c + 8, 4), v(o, 20, 22))
+        ts(v("loff", par, 32, 2), v(o, 0, 16), 32.0 * par, A.add)
     quant(v("xq", 0, 256), v("xs", 0, 256), v("xt0", 0, 1024))
     quant(v("xq", 256, 512), v("xs", 256, 512), v("xt0", 1024, 2048))
     ts(v("si", 64, 96), D, 3, A.logical_shift_right, 31, A.bitwise_and)
@@ -292,7 +285,8 @@ def rank_program(g, core, T, topo):
 
     for r in range(R):
         xt, xh, cq, cs, xn = "xt%d" % r, "xh%d" % r, "cq%d" % r, "cs%d" % r, "xt%d" % (r + 1)
-        mm(v("ps0"), v("uq"), v("us"), v("xq"), v("xs"))
+        for h in range(2):
+            mm(v("ps%d" % h, 0, 256), v("u2"), v("s2"), v("xq", 256 * h, 256 * h + 256), v("xs", 256 * h, 256 * h + 256))
         tt(v("gz"), ind(v("zz", 0, 8), GL), v("kk", 0, 64), A.is_ge)
         ts(v("pen", 0, 32), v("gz", 0, 32), BIG, A.mult)
         tt(v("gd"), v("gz", 32, 64), v("gz", 0, 32), A.is_ge)
@@ -301,23 +295,22 @@ def rank_program(g, core, T, topo):
         for t in range(4):
             for h in range(2):
                 act(v(xh, PL * t + 512 * h, PL * t + 512 * h + 512, 2), v(xt, 1024 * h + t, 1024 * h + 1024, 4), 2.0)
-        for k in range(8):
-            tr(v("tt", 64 * k, 64 * k + 64), v("ps0", k, 512, 8))
-        cp(v("sc"), ind(v("tt"), CL))
-        scan(v("pm"), v("rst", 0, 64), v("sc"), A.add, A.min)
+        for h in range(2):
+            for k in range(8):
+                tr(v("tt", 256 * h + k, 256 * h + 256, 8), v("ps%d" % h, k, 256, 8))
+        for c in (0, 32):
+            scan(v("pm", c, c + 32), v("rst", 0, 32), v("tt", 240, 272), A.add, A.min)
         tt(v("ge"), ind(v("pm", 0, 32), BL), v("pm", 32, 64), A.is_ge)
         scan(v("wb", 0, 32), v("rm"), v("ge"), A.mult, A.add)
         tt(v("a1"), ind(v("wb", 0, 32), AL), v("ab"), A.subtract)
         tr(v("a2"), v("a1"))
         tt(v("a3"), v("a2", 0, 32, 2), v("a2", 1, 32, 2), A.min)
         ts(v("aoff"), v("a3"), -4.0, A.mult)
-        if A_SPLIT < 16:
-            act(v("at", 16 * A_SPLIT, 256), ind(v(xt), v("aoff", A_SPLIT, 16)))
-        if A_SPLIT:
-            cp(v("at", 0, 16 * A_SPLIT), ind(v(xt), v("aoff", 0, A_SPLIT)))
+        act(v("at", 16 * A_SPLIT, 256), ind(v(xt), v("aoff", A_SPLIT, 16)))
+        cp(v("at", 0, 16 * A_SPLIT), ind(v(xt), v("aoff", 0, A_SPLIT)))
         quant(v(cq, 64, 192), v(cs, 64, 192), v("at"))
         sender(r)
-        tt(v("ms"), ind(v("sc", 0, 32), ML), v("pen"), A.add)
+        tt(v("ms"), ind(v("tt", 240, 272), ML), v("pen"), A.add)
         scan(v("low"), v("rst"), v("ms"), A.add, A.min)
         tt(v("mx"), v("low", 7, 64, 8), v("low", 39, 96, 8), A.max)
         tt(v("fl", 0, 16), ind(v("wb", 0, 32), CD), v("zz"), A.is_gt)
@@ -357,13 +350,8 @@ def rank_program(g, core, T, topo):
         for b in range(4):
             act(v("gt", b, 256, 4), v("ps%d" % b, 0, 64), 2.0 ** -6)
         for t in range(4):
-            if SUM_BY_LIST:
-                for a in range(0, 512, SUM_BY_LIST):
-                    b = a + SUM_BY_LIST
-                    tt(v(xh, PL * t + 2 * a + 1, PL * t + 2 * b, 2), ind(v("mg"), v("soff", 32 * t + a // 16, 32 * t + b // 16)), v(xt, 4 * a + t, 4 * b, 4), A.add)
-            else:
-                for k in range(1, 8):
-                    tt(v(xh, PL * t + 2 * k + 1, PL * t + 1024, 16), v(xt, 4 * k + t, 2048, 32), v("mg", t, 256, 4), A.add)
+            for k in range(1, 8):
+                tt(v(xh, PL * t + 2 * k + 1, PL * t + 1024, 16), v(xt, 4 * k + t, 2048, 32), v("mg", t, 256, 4), A.add)
         tt(v("df", 8, 16), v("df", 0, 8), NN, A.mult)
         tt(v("zz", 0, 8), v("zz", 0, 8), v("df", 8, 16), A.add)
         if r < R - 1:
@@ -381,13 +369,13 @@ def rank_program(g, core, T, topo):
         tt(v("en", 128, 160), v("en", 96, 128), v("en", 32, 64), A.max)
         ts(v("em16"), v("en", 128, 160), 2.0, A.mult)
         quant(v("gq"), v("gs"), v("gt"))
-        for b in range(4):
+        for b in (0, 2, 1, 3):
             mm(v("ps%d" % (4 + b), 0, 128), v("wq", 128 * b, 128 * b + 128), v("wp", 128 * b, 128 * b + 128), v("gq"), v("gs"), False, True)
         for b in range(4):
             act(v(xh, PL * b + 1024, PL * b + PL), v("ps%d" % (4 + b), 0, 64), 2.0 ** -5)
         if r == R - 1:
             for h in range(2):
-                z0, z1 = v("zz", 2 * h, 8, 4), v("zz", 2 * h + 1, 8, 4)
+                z0, z1 = v("zz", 4 * h, 4 * h + 4, 2), v("zz", 4 * h + 1, 4 * h + 4, 2)
                 act(v("ht", h, 12, 6), z0, -1.0, 8.0)
                 tt(v("ht", 2 + h, 12, 6), z0, z1, A.subtract)
                 act(v("ht", 4 + h, 12, 6), z1)
@@ -404,7 +392,7 @@ def rank_program(g, core, T, topo):
                     store("s", T.oc[:, 4 * a:4 * b], bytes_of(v("xq", a, b)), v("xq", a, b), 1024 * (512 - a))
                     if b == 512:
                         for k in range(4):
-                            store("s", T.osc[4 * k:4 * k + 4, :], T.xs[32 * k:32 * k + 4, :], v("xs"), 2048)
+                            store("sa"[k // 2], T.osc[4 * k:4 * k + 4, :], T.xs[32 * k:32 * k + 4, :], v("xs"), 2048)
             elif kind == "y":
                 (cp if t == "v" else act)(v("yb", a, b), v(bank[a], 0, b - a))
                 store("a", T.y[:, a:b], v("yb", a, b)[0], v("yb", a, b), 1024 * (512 - a) - 512 * (b - a))

from concourse.mybir import dt, AluOpType, ActivationFunctionType

F32, BF, I32, U16, U8, CODE = "float32", "bfloat16", "int32", "uint16", "uint8", "float8_e4m3fn_x4"
R = 3
PL = 1088
BIG = 2.0 ** 99
FAR = 2.0 ** 20
PLAN = [s for a in (0, 256) for s in (("v", 0, a, a + 256), ("a", 2, a, a + 256), ("v", 1, a, a + 256), ("a", 3, a, a + 256), ("q", 0, a, a + 256))]
LAST = [s for a in (0, 128, 256, 384) for s in (("v", 0, a, a + 128), ("a", 2, a, a + 128), ("v", 1, a, a + 128), ("a", 3, a, a + 128),
                                                ("q", a // 128, a, a + 128), ("y", "v" if a == 384 else "a", a, a + 128))]
A_SPLIT = 6
EST = {"cyc": 1.0, "wake": 100.0, "gath": 1.56, "tt2": 1.0, "pe": 0.7, "dma": 1800.0, "bw": 280.0, "far": 2800.0, "first": 2000.0}


def _sb(n, t):
    return ("sbuf", [128, n], t)


SCRATCH = {
    "ub": _sb(512, BF), "vb": _sb(512, BF), "uq": _sb(128, CODE), "us": _sb(128, U8), "vq": _sb(128, CODE), "vs": _sb(128, U8),
    "wq": _sb(512, CODE), "wp": _sb(512, U8), "ec": _sb(528, BF), "eb": _sb(528, BF), "eq": _sb(512, CODE), "es": _sb(512, U8),
    "xq": _sb(512, CODE), "xs": _sb(512, U8), "at": _sb(512, BF), "gt": _sb(512, BF), "gq": _sb(128, CODE), "gs": _sb(128, U8),
    "mg": _sb(256, BF), "yb": _sb(512, F32), "c6": _sb(64, F32), "y4": _sb(64, F32), "mb": _sb(64, F32), "moff": _sb(16, U16),
    "src": _sb(48, I32), "si": _sb(96, I32), "sf": _sb(64, F32), "ta": _sb(48, F32), "tb": _sb(48, F32), "o0": _sb(32, F32), "o1": _sb(32, F32),
    "pi": _sb(1, I32), "bi": _sb(8, I32), "bf": _sb(16, F32), "cc": _sb(24, F32), "kk": _sb(96, F32), "rst": _sb(96, F32), "rm": _sb(32, F32),
    "c4": _sb(32, F32), "yp": _sb(32, F32), "ab": _sb(32, F32), "off": _sb(32, U16), "loff": _sb(32, U16), "aoff": _sb(16, U16), "em16": _sb(32, U16),
    "st": _sb(128, F32), "p4": _sb(128, BF), "zs": _sb(64, BF), "tt": _sb(512, F32), "pm": _sb(64, F32), "ge": _sb(32, F32), "wb": _sb(48, F32),
    "a1": _sb(32, F32), "a2": _sb(32, F32), "a3": _sb(16, F32), "m1": _sb(64, F32), "m2": _sb(64, F32), "m3": _sb(48, F32),
    "pen": _sb(96, F32), "gz": _sb(64, F32), "gd": _sb(32, F32), "ms": _sb(96, F32), "low": _sb(96, F32),
    "mx": _sb(8, F32), "l0": _sb(4, F32), "fl": _sb(24, F32), "zz": _sb(16, F32), "pr": _sb(16, F32), "dd": _sb(48, F32), "up": _sb(32, F32),
    "pb": _sb(128, BF), "tab": _sb(128, BF), "pg": _sb(512, BF), "pt": _sb(512, BF), "e2": _sb(320, BF), "en": _sb(160, F32),
    "df": _sb(16, F32), "ht": _sb(32, F32), "ho": _sb(32, F32), "u2": _sb(128, CODE), "s2": _sb(128, U8), "uoff": _sb(8, U16), "cu": _sb(8, F32),
}
for _r in range(R + 1):
    SCRATCH["xt%d" % _r] = _sb(2048, BF)
for _r in range(R):
    SCRATCH["xh%d" % _r] = _sb(4 * PL, BF)
    SCRATCH["cq%d" % _r] = _sb(192, CODE)
    SCRATCH["cs%d" % _r] = _sb(192, U8)
for _b in range(8):
    SCRATCH["ps%d" % _b] = ("psum", [128, 512], F32)

SEMAPHORES = ["sv", "sa", "sp", "sg", "lx0", "lx1", "lh", "ld", "lu", "lw", "ls", "lv", "sto", "sent", "arr0", "arr1", "arr2"]
ORDER = {}


def schedule(ops):
    n = len(ops)
    after = [[] for _ in range(n)]
    for i, o in enumerate(ops):
        for j in o["deps"]:
            after[j].append(i)
    tail = [0.0] * n
    for i in range(n - 1, -1, -1):
        tail[i] = ops[i]["lat"] + max([tail[k] + (EST["wake"] if ops[k]["deps"][i] else 0.0) for k in after[i]] + [0.0])
    left = [len(o["deps"]) for o in ops]
    ready = {i: 0.0 for i in range(n) if left[i] == 0}
    free, end, out = {}, [0.0] * n, []
    while ready:
        start = {i: max(t, free.get(ops[i]["q"], 0.0)) for i, t in ready.items()}
        first = min(ready, key=lambda i: (start[i], -tail[i]))
        q, t0 = ops[first]["q"], start[first]
        best = max((i for i in ready if ops[i]["q"] == q and start[i] <= t0), key=lambda i: tail[i])
        s = start[best]
        free[q] = s + ops[best]["busy"]
        end[best] = s + ops[best]["lat"]
        out.append(best)
        del ready[best]
        for k in after[best]:
            left[k] -= 1
            if left[k] == 0:
                ready[k] = max(end[j] + EST["wake"] if w else end[j] - ops[j]["lat"] for j, w in ops[k]["deps"].items())
    return out


def rank_program(g, core, T, topo):
    rank = T.rank_of(core)
    if rank is None:
        return
    A = AluOpType
    ACT = ActivationFunctionType
    n_ranks = len(T.cores)
    nxt = T.cores[(rank + 1) % n_ranks]
    eng = {"v": g.vector, "a": g.scalar, "p": g.tensor, "g": g, "s": g.sync}
    own = {"v": "sv", "a": "sa", "p": "sp", "g": "sg"}
    ops, hist = [], {}
    planned = "order" in ORDER
    cyc = EST["cyc"]

    def v(name, a=0, b=None, s=1):
        if b is None:
            b = SCRATCH[name][1][1]
        return (T[name][:, a:b:s] if s > 1 else T[name][:, a:b], [(name, range(a, b, s))], len(range(a, b, s)), False, SCRATCH[name][2] == BF)

    def ind(win, off):
        return (win[0].indirect(off[0]), win[1] + off[1], 16 * off[2], True, win[4])

    def add(q, fn, outs, ins, busy, lat=None, free=False, sem=None):
        deps = {}
        if not planned:
            for views, w in ((ins, False), (outs, True)):
                for name, el in [s for x in views for s in x[1]]:
                    el = frozenset(el)
                    for el2, w2, j in hist.get(name, []):
                        if j == len(ops):
                            continue
                        if name.startswith("ps"):
                            if ops[j]["q"] != q or ((w or w2) and not free):
                                deps[j] = True
                            elif w or w2:
                                deps.setdefault(j, False)
                        elif (w or w2) and not el.isdisjoint(el2):
                            deps[j] = True
                    hist.setdefault(name, []).append((el, w, len(ops)))
        ops.append({"q": q, "fn": fn, "deps": deps, "busy": busy, "lat": busy if lat is None else lat, "sem": sem})

    def cost(o, ins, per):
        if any(i[3] for i in ins):
            return 55.0 + EST["gath"] * o[2] * cyc
        return max(64.0, per * o[2]) * cyc

    queued = [EST["dma"]]

    def load(q, out, in_, sem, nbytes, codes=False):
        queued[0] += nbytes / EST["bw"]
        add(q, lambda: eng[q].dma_start(out[0].bitcast(dt.uint8) if codes else out[0], in_), [out], [], 60.0, queued[0], sem=(sem, 16))

    def store(q, out, in_, view, nbytes):
        add(q, lambda: eng[q].dma_start(out, in_), [], [view], 60.0, EST["dma"] + nbytes / EST["bw"], sem=("sto", 16))

    def tt(o, a, b, alu):
        add("v", lambda: g.vector.tensor_tensor(o[0], a[0], b[0], alu), [o], [a, b], cost(o, [a], EST["tt2"] if o[4] and a[4] and b[4] else 2))

    def ts(o, a, s1, op0, s2=None, op1=None):
        ins = [a] + [s for s in (s1, s2) if isinstance(s, tuple)]
        x1 = s1[0] if isinstance(s1, tuple) else s1
        x2 = s2[0] if isinstance(s2, tuple) else s2
        if op1 is None:
            add("v", lambda: g.vector.tensor_scalar(o[0], a[0], x1, None, op0), [o], ins, cost(o, [a], 1))
        else:
            add("v", lambda: g.vector.tensor_scalar(o[0], a[0], x1, x2, op0, op1), [o], ins, cost(o, [a], 1))

    def cp(o, a):
        add("v", lambda: g.vector.tensor_copy(o[0], a[0]), [o], [a], cost(o, [a], 1))

    def tr(o, a):
        add("v", lambda: g.vector.transpose(o[0], a[0]), [o], [a], cost(o, [a], 0.5 if o[4] else 1))

    def scan(o, d0, d1, op0, op1):
        add("v", lambda: g.vector.tensor_tensor_scan(o[0], d0[0], d1[0], 0.0, op0, op1), [o], [d0, d1], cost(o, [], 1))

    def fill(o, c):
        add("v", lambda: g.vector.memset(o[0], c), [o], [], cost(o, [], 0.5))

    def quant(c, s, t):
        add("v", lambda: g.vector.quantize_mx(c[0], s[0], t[0]), [c, s], [t], (12 + 0.22 * t[2]) * cyc / 0.83)

    def act(o, a, scale=None, bias=None):
        if bias is not None:
            add("a", lambda: g.scalar.activation(o[0], a[0], ACT.Identity, bias=bias, scale=scale), [o], [a], cost(o, [a], 1))
        elif scale is None:
            add("a", lambda: g.scalar.activation(o[0], a[0], ACT.Copy), [o], [a], cost(o, [a], 1))
        else:
            add("a", lambda: g.scalar.activation(o[0], a[0], ACT.Copy, scale=scale), [o], [a], cost(o, [a], 1))

    def mm(o, lq, ls, rq, rs, start=True, stop=True):
        add("p", lambda: g.tensor.matmul_mx(o[0], lq[0], ls[0], rq[0], rs[0], start, stop), [o], [lq, ls, rq, rs], (o[2] + 16) * EST["pe"], free=not start)

    def iota(o, pattern, base, cm, flt=True):
        if flt:
            add("g", lambda: g.iota(o[0], pattern, base, cm, allow_small_or_imprecise_dtypes=True), [o], [], 130 + 2 * o[2] * cyc)
        else:
            add("g", lambda: g.iota(o[0], pattern, base, cm), [o], [], 130 + 2 * o[2] * cyc)

    def bytes_of(view):
        return view[0].bitcast(dt.uint8)

    load("a", v("src", 32, 44), T.hg[:, :], "lh", 6144)
    load("a", v("src", 0, 32), T.dg[:, :], "ld", 16384)
    load("s", v("xt0", 0, 1024), T.x[:, 0:1024], "lx0", 262144)
    load("a", v("ub"), T.u[:, :], "lu", 131072)
    load("s", v("xt0", 1024, 2048), T.x[:, 1024:2048], "lx1", 262144)
    load("s", v("wq"), T.wc[:, :], "lw", 262144, codes=True)
    load("s", v("wp"), T.ws[:, :], "ls", 65536)
    load("s", v("vb"), T.v[:, :], "lv", 131072)
    n_loads = len(ops)

    fill(v("ec"), 64.0)
    iota(v("pi"), [[0, 1]], 0, 1, flt=False)
    iota(v("cc", 0, 6), [[0, 3], [16, 2]], 0, 0)
    iota(v("cc", 6, 14), [[0, 2], [4, 2], [16, 2]], 0, 0)
    iota(v("kk"), [[0, 12], [-1, 8]], 8, 0)
    iota(v("c4"), [[0, 4], [1024, 2], [1, 4]], 32, 0)
    iota(v("yp"), [[0, 2], [1, 2], [0, 8]], 0, 0)
    iota(v("cc", 16, 20), [[1, 4]], 36, 0)
    iota(v("cu"), [[2, 4], [0, 2]], 0, 0)
    iota(v("c6"), [[1024, 2], [0, 8], [1, 4]], 28, 0)
    iota(v("y4"), [[0, 4], [1, 4], [0, 4]], 0, 0)
    add("g", lambda: g.affine_select(v("eb")[0], v("ec")[0], [[-1, 528]], A.is_equal, 0.0, 3, 4), [v("eb")], [v("ec")], 170 + 1056 * cyc)
    act(v("sf", 44, 64), v("ec", 0, 20), 0.0)
    act(v("at", 256, 512), v("ec", 0, 256), 0.0)
    act(v("gt", 256, 512), v("ec", 0, 256), 0.0)
    act(v("pb"), v("ec", 0, 128), 0.0)
    act(v("ht"), v("ec", 0, 32), 0.0)
    act(v("zs"), v("ec", 0, 64), 0.0)
    for r in range(R):
        act(v("xh%d" % r, 1, 4 * PL, 16), v("ec", 0, 4 * PL // 16), 0.0)
    for i, m in enumerate((7, 8, 4, 6, 31, 1, 3)):
        ts(v("bi", i, i + 1), v("pi"), m, A.bitwise_and)
    cp(v("bf", 0, 7), v("bi", 0, 7))
    b7, b8, b4, b6, b31, b1, b3, x0, x1, x2, x3, x4 = (v("bf", i, i + 1) for i in range(12))
    BL, AL, ML, CD, DL, GL, NL = (v("off", a, b) for a, b in ((4, 6), (6, 8), (8, 14), (14, 15), (16, 19), (20, 24), (24, 28)))
    ts(v("rst"), v("kk"), 8.0, A.is_equal, BIG, A.mult)
    ts(x1, b4, 8.0, A.mult, 14.0, A.add)
    ts(x2, b31, 8.0, A.mult)
    ts(x3, b8, 0.5, A.mult, 32.0, A.add)
    ts(x4, b8, 0.125, A.mult, 6.0, A.add)
    ts(v("rm"), v("kk", 0, 32), 8.0, A.not_equal)
    ts(v("uoff"), v("cu"), b1, A.add, 16.0, A.mult)
    ts(BL, v("cc", 0, 2), b8, A.add, 7.0, A.add)
    ts(AL, v("cc", 0, 2), x1, A.add, 0.5, A.mult)
    ts(v("a1"), v("c4"), 0.25, A.mult, x2, A.add)
    ts(v("a2"), v("yp"), b1, A.not_equal, -FAR, A.mult)
    ts(GL, v("cc", 6, 10), b8, A.add, 0.25, A.mult)
    tt(v("ab"), v("a1"), v("a2"), A.add)
    ts(ML, v("cc", 0, 6), b7, A.add, b8, A.add)
    ts(CD, b6, 4.0, A.mult, 7.0, A.add)
    ts(v("off", 16, 17), b6, 0.5, A.mult, x3, A.add)
    ts(v("off", 17, 18), b6, 4.0, A.mult, x4, A.add)
    ts(v("off", 18, 19), b6, 0.5, A.mult, 40.0, A.add)
    cp(NL, v("cc", 16, 20))
    ts(v("m1"), v("c6"), 0.25, A.mult, x2, A.add)
    ts(v("m2"), v("y4"), b3, A.not_equal, -FAR, A.mult)
    tt(v("mb"), v("m1"), v("m2"), A.add)

    PF, PM, HC, SX = (v("st", 32 * i, 32 * i + 32) for i in range(4))
    D = v("src", 0, 32)
    ts(v("si", 0, 32), D, 3, A.logical_shift_right)
    cp(v("sf", 32, 44), v("src", 32, 44))
    ts(v("si", 32, 64), D, 7, A.bitwise_and)
    ts(v("m3", 0, 32), D, 256.0, A.is_ge, 32.0, A.mult)
    tt(v("sf", 0, 32), v("si", 0, 32), v("m3", 0, 32), A.add)
    cp(PF, v("si", 32, 64))
    tr(v("tb", 0, 32), v("sf", 0, 64, 2))
    tr(v("ta", 16, 48), v("sf", 1, 64, 2))
    for i in range(4):
        act(v("p4", i, 128, 4), PF, -1.0, 7.0 if i == 2 else 8.0)
    act(PM, PF, -1.0, 7.0)
    act(v("zs", 0, 64, 2), PF, -2.0, 15.0)
    cp(v("ta", 0, 16), v("tb", 0, 16))
    cp(v("tb", 32, 48), v("ta", 32, 48))
    tr(v("o0"), v("ta", 0, 32))
    tr(v("o1"), v("tb", 16, 48))
    quant(v("uq"), v("us"), v("ub"))
    add("v", lambda: g.vector.tensor_copy(v("u2")[0].bitcast(dt.uint32), v("uq")[0].bitcast(dt.uint32).indirect(v("uoff")[0])), [v("u2")], [v("uq"), v("uoff")], 255.0)
    act(v("s2"), ind(v("us"), v("uoff")))
    for par in range(2):
        o = "o%d" % par
        for c in (0, 8):
            act(v("zz", c + 2 * par, c + 8, 4), v(o, 16, 18), -1.0, 8.0)
            act(v("zz", c + 2 * par + 1, c + 8, 4), v(o, 20, 22))
        ts(v("loff", par, 32, 2), v(o, 0, 16), 32.0 * par, A.add)
    quant(v("xq", 0, 256), v("xs", 0, 256), v("xt0", 0, 1024))
    quant(v("xq", 256, 512), v("xs", 256, 512), v("xt0", 1024, 2048))
    ts(v("si", 64, 96), D, 3, A.logical_shift_right, 31, A.bitwise_and)
    ts(SX, D, 256.0, A.is_ge, 0.5, A.mult)
    ts(HC, v("si", 64, 96), 512.0, A.add)
    tt(HC, HC, SX, A.add)
    quant(v("vq"), v("vs"), v("vb"))
    for b in range(4):
        quant(v("eq", 128 * b, 128 * b + 128), v("es", 128 * b, 128 * b + 128), v("eb", 3 - b, 515 - b))

    n_eng = min(len(topo.engines(T.cores[i], T.cores[(i + 1) % n_ranks])) for i in range(n_ranks))
    mask = sum(1 << e for e in topo.engines(core, nxt)[:n_eng])
    rid, pid, _se = topo.addr(nxt)

    def sender(r):
        cq, cs = "cq%d" % r, "cs%d" % r

        def fn():
            g.remote_dma(bytes_of(v(cq, 0, 64)), bytes_of(v(cq, 64, 128)), T.sem["arr%d" % r], T.sem.sent, pid, rid, mask)
            g.remote_dma(v(cs, 0, 64)[0], v(cs, 64, 128)[0], T.sem["arr%d" % r], T.sem.sent, pid, rid, mask)
        add("g", fn, [v(cq, 0, 64), v(cs, 0, 64)], [v(cq, 64, 128), v(cs, 64, 128)], 600.0, EST["far"] + (EST["first"] if r == 0 else 0.0),
            sem=("arr%d" % r, 2 * n_eng))

    for r in range(R):
        xt, xh, cq, cs, xn = "xt%d" % r, "xh%d" % r, "cq%d" % r, "cs%d" % r, "xt%d" % (r + 1)
        for h in range(2):
            mm(v("ps%d" % h, 0, 256), v("u2"), v("s2"), v("xq", 256 * h, 256 * h + 256), v("xs", 256 * h, 256 * h + 256))
        tt(v("gz"), ind(v("zz", 0, 8), GL), v("kk", 0, 64), A.is_ge)
        ts(v("pen", 0, 32), v("gz", 0, 32), BIG, A.mult)
        tt(v("gd"), v("gz", 32, 64), v("gz", 0, 32), A.is_ge)
        ts(v("pen", 64, 96), v("gz", 32, 64), -BIG, A.mult, BIG, A.add)
        ts(v("pen", 32, 64), v("gd"), BIG, A.mult)
        for t in range(4):
            for h in range(2):
                act(v(xh, PL * t + 512 * h, PL * t + 512 * h + 512, 2), v(xt, 1024 * h + t, 1024 * h + 1024, 4), 2.0)
        for h in range(2):
            for k in range(8):
                tr(v("tt", 256 * h + k, 256 * h + 256, 8), v("ps%d" % h, k, 256, 8))
        for c in (0, 32):
            scan(v("pm", c, c + 32), v("rst", 0, 32), v("tt", 240, 272), A.add, A.min)
        tt(v("ge"), ind(v("pm", 0, 32), BL), v("pm", 32, 64), A.is_ge)
        scan(v("wb", 0, 32), v("rm"), v("ge"), A.mult, A.add)
        tt(v("a1"), ind(v("wb", 0, 32), AL), v("ab"), A.subtract)
        tr(v("a2"), v("a1"))
        tt(v("a3"), v("a2", 0, 32, 2), v("a2", 1, 32, 2), A.min)
        ts(v("aoff"), v("a3"), -4.0, A.mult)
        act(v("at", 16 * A_SPLIT, 256), ind(v(xt), v("aoff", A_SPLIT, 16)))
        cp(v("at", 0, 16 * A_SPLIT), ind(v(xt), v("aoff", 0, A_SPLIT)))
        quant(v(cq, 64, 192), v(cs, 64, 192), v("at"))
        sender(r)
        tt(v("ms"), ind(v("tt", 240, 272), ML), v("pen"), A.add)
        scan(v("low"), v("rst"), v("ms"), A.add, A.min)
        tt(v("mx"), v("low", 7, 64, 8), v("low", 39, 96, 8), A.max)
        tt(v("fl", 0, 16), ind(v("wb", 0, 32), CD), v("zz"), A.is_gt)
        tt(v("l0"), v("low", 7, 32, 8), v("mx", 4, 8), A.is_ge)
        tt(v("fl", 17, 24, 2), v("mx", 0, 4), v("low", 71, 96, 8), A.is_ge)
        tt(v("fl", 16, 24, 2), v("l0"), v("fl", 8, 16, 2), A.is_gt)
        tt(v("pr"), v("fl", 8, 24), v("zz"), A.mult)
        tt(v("wb", 32, 40), v("pr", 0, 16, 2), v("pr", 1, 16, 2), A.max)
        tt(v("wb", 40, 44), v("mx", 0, 4), v("mx", 4, 8), A.max)
        tt(v("m1"), ind(v("wb", 0, 44), NL), v("mb"), A.subtract)
        cp(v("dd"), ind(v("wb", 0, 44), DL))
        ZA, ZL, C1, C, MM = (v("dd", 8 * i, 8 * i + 8) for i in range(5))
        B0, B1, HP, T2, BS, NN = (v("pb", i, 128, 16) for i in (0, 4, 8, 12, 1, 9))
        UP, NU, FL, BZ = (v("up", 8 * i, 8 * i + 8) for i in range(4))
        tr(v("m2"), v("m1"))
        tt(v("m3", 0, 32), v("m2", 0, 64, 2), v("m2", 1, 64, 2), A.min)
        tt(v("m3", 32, 48), v("m3", 0, 32, 2), v("m3", 1, 32, 2), A.min)
        ts(v("moff"), v("m3", 32, 48), -4.0, A.mult, 0.0, A.max)
        act(v("mg"), ind(v(xt), v("moff")))
        tt(NN, C1, ZA, A.subtract)
        tt(UP, ZL, C, A.is_lt)
        tt(NU, NN, UP, A.mult)
        ts(FL, MM, BIG / 2, A.is_lt, 0.5, A.mult)
        tt(B0, ZL, NU, A.add)
        tt(BZ, FL, ZA, A.subtract)
        tt(B1, B0, NN, A.subtract)
        tt(HP, ZA, NU, A.add)
        tt(T2, B1, NU, A.add)
        tt(BS, BZ, B0, A.subtract)
        tt(v("df", 0, 8), v("fl", 8, 16), v("fl", 16, 24), A.subtract)
        tr(v("tab"), v("pb"))
        act(v("pg", 0, 256), ind(v("tab"), v("loff", 0, 16)))
        act(v("pg", 256, 512), ind(v("tab"), v("loff", 16, 32)))
        for b in range(8):
            e = b % 4
            mm(v("ps%d" % b, 0, 128), v("eq", 128 * e, 128 * e + 128), v("es", 128 * e, 128 * e + 128), v(cq, 0, 128), v(cs, 0, 128), True, b < 4)
        for b in range(4):
            act(v("gt", b, 256, 4), v("ps%d" % b, 0, 64), 2.0 ** -6)
        for t in range(4):
            for k in range(1, 8):
                tt(v(xh, PL * t + 2 * k + 1, PL * t + 1024, 16), v(xt, 4 * k + t, 2048, 32), v("mg", t, 256, 4), A.add)
        tt(v("df", 8, 16), v("df", 0, 8), NN, A.mult)
        tt(v("zz", 0, 8), v("zz", 0, 8), v("df", 8, 16), A.add)
        if r < R - 1:
            act(v("zz", 8, 16), v("zz", 0, 8))
        tr(v("pt", 0, 256), v("pg", 0, 256))
        tr(v("pt", 256, 512), v("pg", 256, 512))
        tt(v("e2", 0, 128), v("pt", 0, 512, 4), v("p4"), A.is_ge)
        tt(v("e2", 192, 256), v("pt", 1, 512, 8), v("zs"), A.add)
        tt(v("e2", 128, 192), v("e2", 0, 128, 2), v("e2", 1, 128, 2), A.subtract)
        tt(v("en", 0, 32), v("pt", 8, 512, 16), PM, A.is_equal)
        tt(v("e2", 256, 320), v("e2", 128, 192), v("e2", 192, 256), A.mult)
        tt(v("en", 32, 64), v("en", 0, 32), HC, A.mult)
        tt(v("en", 64, 96), v("e2", 256, 320, 2), v("e2", 257, 320, 2), A.add)
        tt(v("en", 96, 128), v("en", 64, 96), D, A.add)
        tt(v("en", 128, 160), v("en", 96, 128), v("en", 32, 64), A.max)
        ts(v("em16"), v("en", 128, 160), 2.0, A.mult)
        quant(v("gq"), v("gs"), v("gt"))
        for b in (0, 2, 1, 3):
            mm(v("ps%d" % (4 + b), 0, 128), v("wq", 128 * b, 128 * b + 128), v("wp", 128 * b, 128 * b + 128), v("gq"), v("gs"), False, True)
        for b in range(4):
            act(v(xh, PL * b + 1024, PL * b + PL), v("ps%d" % (4 + b), 0, 64), 2.0 ** -5)
        if r == R - 1:
            for h in range(2):
                z0, z1 = v("zz", 4 * h, 4 * h + 4, 2), v("zz", 4 * h + 1, 4 * h + 4, 2)
                act(v("ht", h, 12, 6), z0, -1.0, 8.0)
                tt(v("ht", 2 + h, 12, 6), z0, z1, A.subtract)
                act(v("ht", 4 + h, 12, 6), z1)
            tr(v("ho"), v("ht"))
            for a in range(4):
                store("s", T.oh[2 * a:2 * a + 2, :], T.ho[32 * a:32 * a + 12, :], v("ho"), 1536)
        bank = {}
        for kind, t, a, b in (PLAN if r < R - 1 else LAST):
            if kind == "q":
                quant(v("xq", a, b), v("xs", a, b), v(xn, 4 * a, 4 * b))
                if r == R - 1:
                    bank[a] = "ps%d" % t
                    mm(v(bank[a], 0, b - a), v("vq"), v("vs"), v("xq", a, b), v("xs", a, b))
                    store("s", T.oc[:, 4 * a:4 * b], bytes_of(v("xq", a, b)), v("xq", a, b), 1024 * (512 - a))
                    if b == 512:
                        for k in range(4):
                            store("sa"[k // 2], T.osc[4 * k:4 * k + 4, :], T.xs[32 * k:32 * k + 4, :], v("xs"), 2048)
            elif kind == "y":
                (cp if t == "v" else act)(v("yb", a, b), v(bank[a], 0, b - a))
                store("a", T.y[:, a:b], v("yb", a, b)[0], v("yb", a, b), 1024 * (512 - a) - 512 * (b - a))
            else:
                src = ind(v(xh, PL * t, PL * t + PL), v("em16", a // 16, b // 16))
                dst = v(xn, 4 * a + t, 4 * b, 4)
                if kind == "v":
                    ts(dst, src, 0.5, A.mult)
                else:
                    act(dst, src, 0.5)

    if not planned:
        for i in range(1, n_loads):
            prev = [j for j in range(i) if ops[j]["q"] == ops[i]["q"]]
            if prev:
                ops[i]["deps"][prev[-1]] = False
        ORDER["order"] = schedule(ops)
        ORDER["deps"] = [o["deps"] for o in ops]
    count = {"sv": 0, "sa": 0, "sp": 0, "sg": 0, "sto": 0}
    known = {q: {} for q in eng}
    token = {}
    for i in ORDER["order"]:
        o = ops[i]
        q = o["q"]
        for tok in sorted((token[j] for j, w in ORDER["deps"][i].items() if w), key=lambda t: -t[1]):
            if known[q].get(tok[0], 0) < tok[1]:
                eng[q].wait_ge(T.sem[tok[0]], tok[1])
                known[q][tok[0]] = tok[1]
            for s, n in tok[2].items():
                if known[q].get(s, 0) < n:
                    known[q][s] = n
        if o["sem"] is None:
            s = own[q]
            o["fn"]().then_inc(T.sem[s], 1)
            count[s] += 1
            token[i] = (s, count[s], dict(known[q]))
        elif q == "g":
            o["fn"]()
            token[i] = (o["sem"][0], o["sem"][1], {})
        else:
            o["fn"]().then_inc(T.sem[o["sem"][0]], 16)
            if o["sem"][0] == "sto":
                count["sto"] += 16
            token[i] = (o["sem"][0], 16, {})
    g.wait_ge(T.sem.sent, 2 * R * n_eng)
    for s in count:
        g.wait_ge(T.sem[s], count[s])
